import numpy as np, ml_dtypes
CORES = [2,3,42,43,82,83,122,123]
N = 8
BF = ml_dtypes.bfloat16
def f(rng, *shape):
    return (rng.standard_normal(shape, dtype=np.float32) * np.exp2(rng.integers(-2, 3, shape[:-1] + (1,)))).astype(BF)
def wide(rng, *shape):
    v = f(rng, *shape).astype(np.float32); k = shape[:-2] + (1, shape[-1])
    return (v * np.exp2(rng.integers(-6, 7, k)) * (rng.random(k) > 0.0625)).astype(BF)
def gentries(a):
    return np.ascontiguousarray(a.reshape(8, 16, -1).transpose(0, 2, 1)).reshape(8, -1)
def gtable(e):
    e = np.asarray(e); return np.ascontiguousarray(e.reshape(8, -1, 16).transpose(0, 2, 1)).reshape(128, -1).astype(np.int32)
WAY = "abc"; W = len(WAY)
IC, CG, CAPP, TOT, S = 2048, 256, 256, 2048, 512
def numbers(a):
    return np.stack([gentries(u) for u in a])
def slots(a):
    return np.stack([gentries(u) for u in a]).reshape(N, N, CAPP)
def columns(t, a):
    e = slots(a); t = t.astype(np.float64)
    return np.stack([np.concatenate([t[q][:, e[q, r]] for q in range(N)], axis=1) for r in range(N)])
def sums(t, x):
    return np.stack([np.bincount(x, weights=t[o], minlength=TOT) for o in range(16)])
def home(p, a):
    e = slots(a); y = np.zeros((N, 16, IC), np.float64)
    for q in range(N):
        for r in range(N):
            y[q][:, e[q, r]] += p[r][:, q * CAPP:(q + 1) * CAPP]
    return y
def anyslots(rng):
    return np.argsort(rng.random((W, N, N, IC)), axis=-1)[..., :CAPP]
def anynumbers(rng):
    x = rng.integers(0, TOT, (W, N, 8, S)); few = rng.integers(0, TOT, (W, N, 8, 32))
    return np.where(rng.random(x.shape) < 0.5, np.take_along_axis(few, rng.integers(0, 32, x.shape), axis=-1), x)
def make(rng, x, e):
    o = np.argsort(x[0], axis=-1, kind="stable"); x = np.stack([np.take_along_axis(u, o, axis=-1) for u in x])
    ob = np.lexsort((rng.random(x[1].shape), x[1]), axis=-1)
    d = {"f" + c: f(rng, N, 16, IC) for c in WAY}
    d["v"] = (rng.standard_normal((N, 8, S)) * np.exp2(rng.integers(-1, 2, (N, 8, 1)))).astype(np.float32)
    for w, c in enumerate(WAY): d["x" + c] = np.stack([gtable(u) for u in x[w]])
    d["ob"] = np.stack([gtable(u) for u in ob])
    for w, c in enumerate(WAY): d["l" + c] = np.stack([gtable(u.reshape(8, CG)) for u in e[w]])
    return d
def setup_inputs(rng):
    return make(rng, anynumbers(rng), anyslots(rng))
def setup_inputs_runs(rng):
    x = anynumbers(rng); h = rng.integers(0, TOT, (W, N, 8, 1))
    for w in range(W): x[w, :, :, w * S // 8:w * S // 8 + S // 2] = h[w]
    x[0, :, 0:2] = h[0, :, 0:1]; x[1, :, 1:3] = h[1, :, 1:2]
    return make(rng, x, anyslots(rng))
def setup_inputs_apart(rng):
    x = np.argsort(rng.random((W, N, 8 * S // TOT, TOT)), axis=-1).reshape(W, N, 8, S)
    return make(rng, x, anyslots(rng))
def setup_inputs_ends(rng):
    x = rng.integers(0, N, (W, N, 8, S)) * CAPP + rng.integers(0, 2, (W, N, 8, S)) * (CAPP - 1)
    x = np.where(rng.random(x.shape) < 0.75, x, rng.integers(0, TOT, x.shape)); x[..., 0] = 0; x[..., 1] = TOT - 1
    e = 1 + np.argsort(rng.random((W, N, N, IC - 2)), axis=-1)[..., :CAPP]; e[..., 0] = IC - 1; e[..., -1] = 0
    return make(rng, x, e)
def setup_inputs_alike(rng):
    x = anynumbers(rng); x[:, :, 1:] = x[:, :, :1].copy()
    e = np.repeat(np.argsort(rng.random((W, N, 1, IC)), axis=-1)[..., :CAPP], N, axis=2)
    return make(rng, x, e)
def setup_inputs_spread(rng):
    d = setup_inputs(rng)
    for c in WAY[1:]: d["f" + c] = wide(rng, N, 16, IC)
    return d
def check_inputs(d):
    bad = []
    for c in WAY:
        x = numbers(d["x" + c]); e = slots(d["l" + c])
        if not np.isfinite(d["f" + c].astype(np.float32)).all(): bad.append("finite_f" + c)
        if x.min() < 0 or x.max() >= TOT: bad.append("range_x" + c)
        if e.min() < 0 or e.max() >= IC: bad.append("range_l" + c)
        if (np.diff(np.sort(e, axis=-1), axis=-1) == 0).any(): bad.append("different_l" + c)
    if not np.isfinite(d["v"]).all(): bad.append("finite_v")
    if (np.diff(numbers(d["xa"]), axis=-1) < 0).any(): bad.append("sorted_xa")
    o = numbers(d["ob"])
    if not (np.sort(o, axis=-1) == np.arange(S)).all(): bad.append("places_ob")
    elif (np.diff(np.take_along_axis(numbers(d["xb"]), o, axis=-1), axis=-1) < 0).any(): bad.append("sorted_xb_by_ob")
    return bad
def reference(fa, fb, fc, v, xa, xb, xc, ob, la, lb, lc):
    xi = numbers(xa).reshape(N, 8 * S); xj = numbers(xb).reshape(N, 8 * S)
    w = np.repeat(v.astype(np.float64).reshape(N, 1, 8 * S), 16, axis=1)
    for t, x, a in ((fc, xc, lc),):
        u = columns(t, a); x = numbers(x).reshape(N, 8 * S)
        w = w * np.stack([u[r][:, x[r]] for r in range(N)])
    u = columns(fb, lb)
    ya = fa.astype(np.float64) * home([sums(w[r] * u[r][:, xj[r]], xi[r]) for r in range(N)], la)
    u = columns(ya, la)
    yb = home([sums(w[r] * u[r][:, xi[r]], xj[r]) for r in range(N)], lb)
    return {"ya": ya.astype(np.float32), "yb": yb.astype(np.float32)}

@@ -1,0 +1,498 @@
+import numpy as np
+from concourse.bass import DstId, RemoteDMATransfer
+from concourse.mybir import AluOpType, ActivationFunctionType
+
+OPS = AluOpType
+COPY = ActivationFunctionType.Copy
+F, BFT, I32, U16, F16 = "float32", "bfloat16", "int32", "uint16", "float16"
+
+NDUMP = 640
+SCRATCH = {}
+for _n, _c, _t in [
+        ("i1", 128, I32), ("i1b", 128, I32), ("i2", 8, I32), ("i2b", 8, I32), ("i4", 128, I32),
+        ("i4b", 128, I32), ("i5", 128, I32), ("ki", 32, I32), ("kk", 32, U16), ("dj", 32, F),
+        ("mk", 8, F), ("i16", 512, F), ("z", 144, F), ("z16", 144, F16), ("ident", 128, F), ("mbf", 128, F),
+        ("mbb", 128, BFT), ("e8", 128, F), ("n1", 128, F), ("n2", 128, F), ("p1", 128, F), ("p2", 128, F),
+        ("repb", 1024, BFT), ("repf", 1024, F),
+        ("tf", 2048, BFT), ("far", 2048, BFT), ("v8", 512, F), ("v16", 512, F), ("xi", 128, I32), ("ln", 32, I32),
+        ("laf", 16, F), ("lau", 16, U16), ("lbu", 16, U16), ("lu", 32, U16), ("lf", 128, U16),
+        ("xu", 64, U16), ("obu", 32, U16), ("xpa", 34, F), ("xpb", 34, F),
+        ("r1", 16, I32), ("r2", 16, I32), ("r3", 16, I32), ("r4", 16, I32), ("r5", 16, I32), ("r6", 16, I32),
+        ("ea", 32, F), ("ca", 32, F), ("da", 32, F), ("fma", 32, F), ("ga", 32, F), ("offa", 32, U16),
+        ("eb", 32, F), ("cb2", 32, F), ("db", 32, F), ("fmb", 32, F), ("gb", 32, F), ("offb", 32, U16),
+        ("exa", 512, BFT), ("exb", 512, BFT),
+        ("pk0", 32, F), ("pk", 32, F), ("exp", 512, F), ("fp", 512, F), ("pm", 512, F), ("pm2", 256, F),
+        ("pm4", 128, F), ("pm8", 64, F), ("pint", 32, I32),
+        ("xao", 32, I32), ("xbo", 32, I32), ("u1", 32, I32), ("u2", 32, I32), ("u3", 32, I32), ("u4", 32, I32),
+        ("u5", 32, I32), ("u6", 32, I32), ("xaou", 32, U16),
+        ("s1", 512, BFT), ("land1", 512, BFT), ("tb", 2048, BFT), ("tc", 2048, BFT), ("vc", 512, F), ("vcp", 512, F),
+        ("wa", 512, F), ("ra", 512, F), ("w1", 2048 + NDUMP, F), ("s3", 224, F), ("q3", 256, F), ("fan", 256, F),
+        ("w2", 2048, F), ("gt", 2048, F), ("ya1", 256, F), ("ya2", 256, F),
+        ("s5", 224, F), ("land3", 256, F), ("land5", 256, F), ("land6", 256, F), ("ta", 2048, F), ("wb", 512, F),
+        ("rb", 512, F), ("w3", 2048 + NDUMP, F), ("s6", 224, F), ("q6", 256, F), ("w4", 2048, F), ("yb2", 256, F)]:
+    SCRATCH[_n] = ("sbuf", [128, _c], _t)
+SCRATCH["ll"] = ("sbuf", [128, 8, 4], I32)
+SCRATCH["rr"] = ("sbuf", [128, 8, 8, 4], F16)
+SCRATCH["rra"] = ("sbuf", [128, 128], F)
+for _k in range(8):
+    SCRATCH["ps%d" % _k] = ("psum", [128, 512], F)
+NSEM = 130
+SEMAPHORES = ["e%d" % k for k in range(NSEM)] + ["arr%d%s" % (k, s) for k in (1, 3, 5, 6) for s in "fhsn"] + ["sent"]
+
+
+def rank_program(g, core, T, topo):
+    me = T.rank_of(core)
+    if me is None:
+        return
+    cores = list(T.cores)
+    here = topo.chip(core)
+    queues = {"v": g.vector, "s": g.scalar, "t": g.tensor, "g": g, "y": g.sync}
+
+    ops = []
+    hist = {}
+    groups = {}
+
+    def record(q, f, outs, ins, grp=None, inc=1, fixed=None):
+        k = len(ops)
+        dep = set()
+        touched = []
+        for w, side in ((1, outs), (0, ins)):
+            for pair in side:
+                for reg in pair[1]:
+                    touched.append((w, reg))
+        for w, reg in touched:
+            n, a, b, lo, hi = reg
+            for (j, w2, a2, b2, lo2, hi2) in hist.get(n, []):
+                if n[:2] == "ps":
+                    if ops[j]["q"] == q:
+                        if q != "t" and (w or w2) and lo < hi2 and lo2 < hi:
+                            dep.add(j)
+                    else:
+                        dep.add(j)
+                elif (w or w2) and lo < hi2 and lo2 < hi and a < b2 and a2 < b:
+                    dep.add(j)
+        for w, reg in touched:
+            hist.setdefault(reg[0], []).append((k, w) + tuple(reg[1:]))
+        if grp is not None:
+            groups.setdefault(grp, []).append(k)
+        dep.discard(k)
+        ops.append({"q": q, "f": f, "dep": dep, "grp": grp, "inc": inc, "fixed": fixed})
+        return k
+
+    def A(n, lo=0, hi=None, p0=0, p1=128, step=1):
+        hi = SCRATCH[n][1][1] if hi is None else hi
+        return (T[n][p0:p1, lo:hi] if step == 1 else T[n][p0:p1, lo:hi:step], [(n, p0, p1, lo, hi)])
+
+    def X(ap, n, lo, hi):
+        return (ap, [(n, 0, 128, lo, hi)])
+
+    def ind(win, off):
+        return (win[0].indirect(off[0]), win[1] + off[1])
+
+    def cp(q, out, in_, grp=None):
+        if q == "v":
+            record(q, lambda: g.vector.tensor_copy(out[0], in_[0]), [out], [in_], grp)
+        else:
+            record(q, lambda: g.scalar.activation(out[0], in_[0], COPY), [out], [in_], grp)
+
+    def scaled(out, in_, s, grp=None):
+        record("s", lambda: g.scalar.activation(out[0], in_[0], COPY, scale=s[0]), [out], [in_, s], grp)
+
+    def tt(out, a, b, o, grp=None):
+        record("v", lambda: g.vector.tensor_tensor(out[0], a[0], b[0], o), [out], [a, b], grp)
+
+    def ts(out, a, s1, o1, s2=None, o2=None, grp=None):
+        ins = [a] + [s for s in (s1, s2) if isinstance(s, tuple)]
+        v1 = s1[0] if isinstance(s1, tuple) else s1
+        v2 = s2[0] if isinstance(s2, tuple) else s2
+        if o2 is None:
+            record("v", lambda: g.vector.tensor_scalar(out[0], a[0], v1, None, o1), [out], ins, grp)
+        else:
+            record("v", lambda: g.vector.tensor_scalar(out[0], a[0], v1, v2, o1, o2), [out], ins, grp)
+
+    def fill(out, c, grp=None):
+        record("v", lambda: g.vector.memset(out[0], c), [out], [], grp)
+
+    def turn(out, in_):
+        record("v", lambda: g.vector.transpose(out[0], in_[0]), [out], [in_])
+
+    def mm(out, l, r, start, stop, grp):
+        record("t", lambda: g.tensor.matmul(out[0], l[0], r[0], start, stop), [out], [l, r], grp)
+
+    def iota(n, cols, pattern, base, cm, fl=False):
+        out = A(n, 0, cols)
+        if fl:
+            record("g", lambda: g.iota(out[0], pattern, base, cm, allow_small_or_imprecise_dtypes=True), [out], [])
+        else:
+            record("g", lambda: g.iota(out[0], pattern, base, cm), [out], [])
+
+    def pick(n, base):
+        out, same = A(n), A("mbf")
+        record("g", lambda: g.affine_select(out[0], same[0], [[-1, 128]], OPS.is_equal, 0.0, base, 1), [out], [same])
+
+    def scan(out, keep, x):
+        record("v", lambda: g.vector.tensor_tensor_scan(out[0], keep[0], x[0], 0.0, OPS.mult, OPS.add), [out], [keep, x])
+
+    def dma(q, out, in_, grp, after=()):
+        e = queues[q]
+        record(q, lambda: e.dma_start(out[0], in_[0]), [out], [in_] + list(after), grp, 16)
+
+    def ext(ap, n):
+        return (ap, [("ext_" + n, 0, 128, 0, 1)])
+
+    ranks = range(len(cores))
+
+    def chip(q):
+        return topo.chip(cores[q])
+
+    def row(q):
+        return len([p for p in ranks if p < q and topo.same_plane(chip(p), chip(q))])
+
+    sib = [q for q in ranks if q != me and chip(q) == here]
+    near = [q for q in ranks if topo.same_plane(chip(q), here)]
+    others = [q for q in ranks if q != me and q not in sib and q not in near]
+    far0 = [q for q in others if row(q) == row(me)]
+    far1 = [q for q in others if q not in far0]
+    order = far0 + far1 + sib + near + [me]
+    p_own, p_far0, p_far1, p_near = min(sib + [me]), min(far0), min(far1), min(near)
+    kinds = (("s", sib), ("f", far0), ("h", far1), ("n", near))
+
+    off_chip = topo.engines(core, cores[others[0]])
+    on_chip = [e for e in topo.engines(core, cores[sib[0]]) if e not in off_chip]
+
+    def engines_for(q, dests):
+        if q in sib:
+            return on_chip[:len(on_chip) // 2]
+        dests = [d for d in dests if d not in sib]
+        n = len(off_chip) // len(dests)
+        i = dests.index(q)
+        return off_chip[i * n:(i + 1) * n]
+
+    sent = [0]
+
+    def send(src, width, dst, arr, calls):
+        for dests in calls:
+            tr, rd = [], []
+            for q in dests:
+                d = order.index(q)
+                s = A(src, d * width, (d + 1) * width)
+                rd.append(s)
+                rid, pid = topo.addr(cores[q])[:2]
+                es = engines_for(q, dests)
+                sent[0] += len(es)
+                w = [k for k, qs in kinds if q in qs][0]
+                tr.append(RemoteDMATransfer(dst_ids=[DstId(rid=rid, pnc=pid)], dma_engine_mask=sum(1 << e for e in es),
+                                            remote_sem=T.sem[arr + w], srcs=[s[0]],
+                                            dsts=[T[dst][:, width * me:width * me + width]]))
+            record("g", lambda tr=tr: g.remote_dma_fused(tr, local_sem=T.sem["sent"]), [], rd)
+
+    def arrival(n, width, arr, calls):
+        for w, srcs in kinds:
+            regs = [(n, 0, 128, q * width, (q + 1) * width) for q in srcs]
+            num = sum(len(engines_for(q, dests)) for dests in calls for q in dests if q in srcs)
+            record("in_" + arr + w, None, [(None, regs)], [], fixed=(arr + w, num))
+
+    calls1 = (far0 + far1, near + sib)
+    calls3 = (far0, far1, near + sib)
+    calls5 = (far0, far1 + sib, near)
+
+    dma("y", X(T["ll"][:, 0:4, :], "ll", 0, 16), ext(T["lb"][:, :], "lb"), "d_l")
+    dma("s", X(T["ll"][:, 4:8, :], "ll", 16, 32), ext(T["lc"][:, :], "lc"), "d_l")
+    for k in range(8):
+        n = "fb" if k < 4 else "fc"
+        dma("ys"[k % 2], A("tf", 0, 2048, 16 * k, 16 * k + 16), ext(T[n][:, :], n), "d_tf")
+    for k, n in enumerate(("xa", "xb", "xc", "ob")):
+        dma("y", A("xi", 32 * k, 32 * k + 32), ext(T[n][:, :], n), "d_x")
+    dma("y", A("v8", 0, 512, 0, 8), ext(T["v"][:, :], "v"), "d_x")
+    dma("y", A("ln", 0, 16), ext(T["la"][:, :], "la"), "d_x")
+    dma("y", A("ln", 16, 32), ext(T["lb"][:, :], "lb"), "d_x")
+
+    iota("i2", 8, [[-16, 8]], 0, 1)
+    iota("i1", 128, [[0, 8], [-1, 16]], 16, 1)
+    iota("i4", 128, [[-16, 8], [0, 16]], 0, 1)
+    iota("i5", 128, [[1, 8], [0, 16]], 0, -1)
+    iota("dj", 32, [[16, 32]], 2048, 1, True)
+    iota("ki", 32, [[1, 32]], 0, 0)
+    fill(A("z"), 0.0)
+    ts(A("i2b"), A("i2"), 4, OPS.arith_shift_right)
+    ts(A("mk"), A("i2b"), 0, OPS.is_equal)
+    ts(A("i1b"), A("i1"), 15, OPS.bitwise_and)
+    ts(A("i16", 0, 128), A("i1b"), 0, OPS.is_equal)
+    cp("v", A("z", 112, 128), A("i16", 0, 16))
+    ts(A("i4b"), A("i4"), 4, OPS.arith_shift_right)
+    cp("v", A("z16"), A("z"))
+    ts(A("mbf"), A("i4b"), 0, OPS.is_equal)
+    for n, k in (("n1", -1), ("n2", 15), ("p1", 1), ("p2", -15)):
+        pick(n, k)
+    for h in range(8):
+        scaled(A("repb", 128 * h, 128 * h + 128), A("i16", 0, 128), A("mk", h, h + 1), "g_repb")
+
+    for d in range(8):
+        r = order[d]
+        ts(X(T["rr"][:, :, d, :], "rr", d, d + 1), X(T["ll"][:, :, :], "ll", 0, 32), A("mk", r, r + 1), OPS.mult,
+           grp="g_rr")
+    for h in range(8):
+        b = 32 * (h // 2)
+        mm((T["ps4"][b:b + 32, 0:32], [("ps4", b, b + 32, 0, 32)]), A("z16", 112 - 16 * (h % 2), 144 - 16 * (h % 2)),
+           X(T["rr"][:, h, :, :], "rr", 0, 8), h % 2 == 0, h % 2 == 1, "g_lt")
+    fill(A("xpa"), -1.0)
+    cp("v", A("mbb"), A("mbf"))
+    cp("v", A("lu"), A("ps4", 0, 32))
+    fill(A("xpb"), -1.0)
+    cp("v", A("kk"), A("ki"))
+    ts(A("e8"), A("i5"), 0, OPS.is_equal)
+    cp("v", A("s1", 0, 256), ind(A("tf"), A("lu", 0, 16)))
+    cp("s", A("s1", 256, 512), ind(A("tf"), A("lu", 16, 32)))
+    send("s1", 64, "land1", "arr1", calls1)
+    pick("ident", 0)
+    iota("w1", 2048, [[0, 2048]], 0, 0, True)
+    rep, zero = A("repf"), A("w1", 0, 1024)
+    record("g", lambda: g.affine_select(rep[0], zero[0], [[-16, 8], [0, 8], [-1, 16]], OPS.not_equal, 1.0, 0, 1),
+           [rep], [zero])
+    iota("w2", 2048, [[0, 2048]], 0, 0, True)
+    cp("s", A("land1", 64 * me, 64 * me + 64), A("s1", 448, 512))
+
+    for k in range(1, 4):
+        cp("s", A("i16", 128 * k, 128 * k + 128), A("i16", 0, 128), "g_i16")
+    cp("v", A("xpa", 1, 33), A("xi", 0, 32))
+
+    def shift(xp, ps, s):
+        mm(A(ps, 0, 32), A("n1"), A(xp, 1, 33), True, False, "g_n" + s)
+        mm(A(ps, 0, 32), A("n2"), A(xp, 2, 34), False, True, "g_n" + s)
+        mm(A(ps, 32, 64), A("p1"), A(xp, 1, 33), True, False, "g_n" + s)
+        mm(A(ps, 32, 64), A("p2"), A(xp, 0, 32), False, True, "g_n" + s)
+
+    def ends(xp, ps, s, off):
+        tt(A("e" + s), A(ps, 0, 32), A(xp, 1, 33), OPS.not_equal)
+        tt(A("fm" + s), A("d" + s), A("e" + s), OPS.mult)
+        tt(A("g" + s), A("fm" + s), A("dj"), OPS.add)
+        cp("v", A(off), A("g" + s))
+
+    def spread(out, x, grp):
+        for i in range(16):
+            scaled(A(out, i, 512, step=16), A(x), A("i16", i, i + 1), grp)
+
+    shift("xpa", "ps7", "a")
+    mm(A("ps5"), A("e8", 0, 128, 0, 8), A("v8", 0, 512, 0, 8), True, True, "g_v")
+    ts(A("pk0"), A("xi", 32, 64), 2048, OPS.mult)
+    tt(A("da"), A("xpa", 1, 33), A("dj"), OPS.subtract)
+    tt(A("ca"), A("ps7", 32, 64), A("xpa", 1, 33), OPS.is_equal)
+    cp("s", A("v16"), A("ps5"))
+    ends("xpa", "ps7", "a", "offa")
+    cp("v", A("xu"), A("xi", 32, 96))
+    tt(A("exa"), ind(A("ca"), A("kk")), A("i16"), OPS.mult)
+    tt(A("pk"), A("pk0"), A("xpa", 1, 33), OPS.add)
+    cp("v", A("obu"), A("xi", 96, 128))
+    cp("v", A("lau"), A("ln", 0, 16))
+    cp("v", A("laf"), A("ln", 0, 16))
+
+    arrival("land1", 64, "arr1", calls1)
+    for k in range(8):
+        dma("y", A("far", 0, 2048, 16 * k, 16 * k + 16), ext(T["fa"][:, :], "fa"), "d_fa",
+            [A("land1", 64 * q, 64 * q + 64) for q in near])
+    for f, q, n, k, e in ((1, p_own, 2, 0, "s"), (0, p_own, 2, 4, "v"), (1, p_far0, 2, 1, "s"),
+                          (1, p_far1, 2, 2, "v"), (0, p_far0, 2, 5, "s"), (0, p_far1, 2, 6, "v"),
+                          (1, p_near, 1, 3, "s"), (1, p_near + 1, 1, 0, "v"), (0, p_near, 2, 7, "s")):
+        for i in range(4 * n):
+            w = 128 * (4 * f + i % 4)
+            lo = 64 * (q + i // 4)
+            mm(A("ps%d" % k, 64 * i, 64 * i + 64), A("repb", w, w + 128), A("land1", lo, lo + 64), True, True,
+               "g_t%d%d" % (k, q))
+        cp(e, A("tb" if f == 0 else "tc", 256 * q, 256 * (q + n)), A("ps%d" % k, 0, 256 * n))
+    mm(A("ps1"), A("mbb"), A("exa"), True, True, "g_ma")
+    tt(A("vc"), ind(A("tc"), A("xu", 32, 64)), A("v16"), OPS.mult)
+    tt(A("wa"), ind(A("tb"), A("xu", 0, 32)), A("vc"), OPS.mult)
+    scan(A("ra"), A("ps1"), A("wa"))
+    cp("v", ind(A("w1"), A("offa")), A("ra"))
+    spread("exp", "pk", "g_exp")
+    mm(A("ps2"), A("mbf"), A("exp"), True, True, "g_fp")
+    cp("s", A("fp"), A("ps2"))
+    cp("s", A("vcp"), ind(A("vc"), A("obu")))
+
+    def add_slabs(w, s, land, arr):
+        for qs, k in ((far0, 0), (far1, 1), (near + sib, 2), ([me], 3)):
+            for q in qs:
+                for b in range(2):
+                    c = 32 * (order.index(q) % 4)
+                    mm(A("ps%d" % k, c + b, c + 32, step=2), A(w, 256 * q + 128 * b, 256 * q + 128 * b + 128),
+                       A("i16", 0, 16), True, True, "g_%s%d" % (w, k))
+        cp("v", A(s, 0, 64), A("ps0", 0, 64))
+        cp("v", A(s, 64, 128), A("ps1", 64, 128))
+        cp("s", A(s, 128, 224), A("ps2", 0, 96))
+        send(s, 32, land, arr, calls3)
+        cp("s", A(land, 32 * me, 32 * me + 32), A("ps3", 96, 128))
+
+    add_slabs("w1", "s3", "land3", "arr3")
+    iota("w3", 2048, [[0, 2048]], 0, 0, True)
+
+    cp("s", A("fan"), ind(A("far"), A("lau")))
+    for d in range(8):
+        r = order[d]
+        scaled(A("rra", 16 * d, 16 * d + 16), A("laf"), A("mk", r, r + 1), "g_rra")
+    mm(A("ps4", 0, 128), A("i16", 0, 128), A("rra"), True, True, "g_lf")
+    tt(A("pm"), ind(A("fp"), A("obu")), A("i16"), OPS.mult)
+    tt(A("pm2"), A("pm", 0, 512, step=2), A("pm", 1, 512, step=2), OPS.add)
+    cp("v", A("lf"), A("ps4", 0, 128))
+    tt(A("pm4"), A("pm2", 0, 256, step=2), A("pm2", 1, 256, step=2), OPS.add)
+    tt(A("pm8"), A("pm4", 0, 128, step=2), A("pm4", 1, 128, step=2), OPS.add)
+    tt(A("pint"), A("pm8", 0, 64, step=2), A("pm8", 1, 64, step=2), OPS.add)
+
+    def to_natural(land, q, pa, pb):
+        mm(A(pa, 0, 128), A(land, 0, 256, step=2), A("ident"), True, True, "g_n0" + land)
+        mm(A(pb, 0, 128), A(land, 1, 256, step=2), A("ident"), True, True, "g_n1" + land)
+        cp("s", A(q, 0, 128), A(pa, 0, 128))
+        cp("v", A(q, 128, 256), A(pb, 0, 128))
+
+    arrival("land3", 32, "arr3", calls3)
+    to_natural("land3", "q3", "ps6", "ps7")
+    tt(ind(A("w2"), A("lau")), A("q3"), A("fan"), OPS.mult)
+    bank = (0, 0, 1, 1, 1, 2, 2, 3)
+    for d in range(8):
+        for lo, hi in ((0, 128), (128, 256)) if d < 2 else ((0, 256),):
+            cp("vsvsvssv"[d], A("gt", 256 * d + lo, 256 * d + hi),
+               ind(A("w2"), A("lf", 16 * d + lo // 16, 16 * d + hi // 16)))
+        for b in range(2):
+            c = 32 * (d % 4) + 16 * b
+            mm(A("ps%d" % bank[d], c, c + 16), A("gt", 256 * d + 128 * b, 256 * d + 128 * b + 128), A("i16", 0, 16),
+               True, True, "g_m%d" % bank[d])
+        if d == 2:
+            turn(A("s5", 0, 64), A("ps0", 0, 64))
+    turn(A("s5", 64, 128), A("ps1", 64, 128))
+    turn(A("s5", 128, 160), A("ps1", 0, 32))
+    turn(A("s5", 160, 224), A("ps2", 32, 96))
+    turn(A("land5", 32 * me, 32 * me + 32), A("ps3", 96, 128))
+    send("s5", 32, "land5", "arr5", calls5)
+    iota("w4", 2048, [[0, 2048]], 0, 0, True)
+
+    ts(A("xbo"), A("pint"), 11, OPS.arith_shift_right)
+    cp("v", A("xpb", 1, 33), A("xbo"))
+    shift("xpb", "ps1", "b")
+    ts(A("xao"), A("pint"), 2047, OPS.bitwise_and)
+    tt(A("db"), A("xpb", 1, 33), A("dj"), OPS.subtract)
+    tt(A("cb2"), A("ps1", 32, 64), A("xpb", 1, 33), OPS.is_equal)
+    spread("exb", "cb2", "g_exb")
+    ends("xpb", "ps1", "b", "offb")
+    ts(A("u1"), A("xao"), 5, OPS.arith_shift_right, 7, OPS.bitwise_and)
+    ts(A("u2"), A("xao"), 8, OPS.arith_shift_right, 1, OPS.bitwise_and)
+    ts(A("u3"), A("u1"), 32, OPS.mult)
+    ts(A("u4"), A("u2"), -224, OPS.mult)
+    tt(A("u5"), A("u3"), A("xao"), OPS.add)
+    tt(A("u6"), A("u4"), A("u5"), OPS.add)
+    cp("v", A("xaou"), A("u6"))
+
+    arrival("land5", 32, "arr5", calls5)
+    for q, k, u0, u1, e in ((p_far0, 5, 0, 8, "v"), (p_own, 4, 0, 8, "s"), (p_far1, 6, 0, 8, "v"),
+                            (p_near, 7, 0, 4, "s"), (p_near, 3, 4, 6, "v"), (p_near, 0, 6, 8, "s")):
+        for u in range(u0, u1):
+            h = 2 * (u % 4) + u // 4
+            mm(A("ps%d" % k, 64 * (u - u0), 64 * (u - u0) + 64), A("repf", 128 * h, 128 * h + 128),
+               A("land5", 32 * q, 32 * q + 64), True, True, "g_u%d" % k)
+        cp(e, A("ta", 256 * q + 64 * u0, 256 * q + 64 * u1), A("ps%d" % k, 0, 64 * (u1 - u0)))
+    mm(A("ps2"), A("mbb"), A("exb"), True, True, "g_mb")
+
+    def sum_a(half, ps):
+        for k in range(8):
+            lo = 1024 * half + 128 * k
+            mm(A(ps, k, 128, step=8), A("w2", lo, lo + 128), A("i16", 0, 16), True, True, "g_ya%d" % half)
+
+    sum_a(0, "ps4")
+    tt(A("wb"), ind(A("ta"), A("xaou")), A("vcp"), OPS.mult)
+    scan(A("rb"), A("ps2"), A("wb"))
+    cp("v", ind(A("w3"), A("offb")), A("rb"))
+    cp("s", A("ya1", 0, 128), A("ps4", 0, 128))
+
+    add_slabs("w3", "s6", "land6", "arr6")
+
+    sum_a(1, "ps5")
+    cp("s", A("ya1", 128, 256), A("ps5", 0, 128))
+    for k in range(2):
+        mm(A("ps%d" % (6 + k), 0, 128), A("ya1", 128 * k, 128 * k + 128), A("ident"), True, True, "g_b%d" % k)
+        cp("s", A("ya2", 128 * k, 128 * k + 128), A("ps%d" % (6 + k), 0, 128))
+        dma("y", ext(T["ya"][:, 1024 * k:1024 * k + 1024], "ya%d" % k), A("ya2", 128 * k, 128 * k + 128), "d_ya")
+    ts(A("r1"), A("ln", 16, 32), 9, OPS.arith_shift_right)
+    ts(A("r2"), A("ln", 16, 32), 31, OPS.bitwise_and)
+    ts(A("r5"), A("ln", 16, 32), 4, OPS.mult)
+    ts(A("r3"), A("r1"), -2016, OPS.mult)
+    ts(A("r4"), A("r2"), -3, OPS.mult)
+    tt(A("r6"), A("r5"), A("r3"), OPS.add)
+    tt(A("lbu"), A("r6"), A("r4"), OPS.add)
+
+    arrival("land6", 32, "arr6", calls3)
+    to_natural("land6", "q6", "ps2", "ps3")
+    cp("v", ind(A("w4"), A("lbu")), A("q6"))
+    for half in range(2):
+        ps = "ps%d" % half
+        for j in range(4):
+            for k in range(2):
+                lo = 1024 * k + 128 * (4 * half + j)
+                mm(A(ps, 32 * j + 16 * k, 32 * j + 16 * k + 16), A("w4", lo, lo + 128), A("i16", 0, 16), True, True,
+                   "g_yb%d" % half)
+        turn(A("yb2", 128 * half, 128 * half + 128), A(ps, 0, 128))
+    for h in range(8):
+        dma("ys"[h % 2], ext(T["yb"][:, 256 * h:256 * h + 256], "yb%d" % h), A("yb2", 0, 256, 16 * h, 16 * h + 16), "d_yb")
+    record("y", None, [], [(None, [("ext_ya%d" % h, 0, 128, 0, 1) for h in range(2)]
+                            + [("ext_yb%d" % h, 0, 128, 0, 1) for h in range(8)])])
+
+    bits = [0] * len(ops)
+    known = {}
+    need = set()
+    for k, o in enumerate(ops):
+        have = known.get(o["q"], 0)
+        waits = []
+        for j in sorted(o["dep"], reverse=True):
+            if have >> j & 1:
+                continue
+            members = groups[ops[j]["grp"]] if ops[j]["grp"] is not None else [j]
+            if k in members:
+                continue
+            assert max(members) < k
+            for m in members:
+                have |= bits[m]
+            waits.append(j)
+            need.add(j)
+        known[o["q"]] = have
+        bits[k] = have | 1 << k
+        o["waits"] = waits
+        o["have"] = have
+    needed_groups = set(ops[j]["grp"] for j in need if ops[j]["grp"] is not None)
+    chains, used, place, group_sem = [], [0], {}, {}
+
+    def fresh():
+        used[0] += 1
+        return "e%d" % (used[0] - 1)
+
+    for k, o in enumerate(ops):
+        if o["fixed"] is not None:
+            place[k] = o["fixed"]
+        elif o["grp"] in needed_groups and o["grp"] is not None:
+            if o["grp"] not in group_sem:
+                group_sem[o["grp"]] = fresh()
+            place[k] = (group_sem[o["grp"]], sum(ops[m]["inc"] for m in groups[o["grp"]]))
+        elif k in need:
+            for c in chains:
+                if c["q"] == o["q"] and o["have"] >> c["last"] & 1:
+                    break
+            else:
+                c = {"q": o["q"], "sem": fresh(), "last": None, "n": 0}
+                chains.append(c)
+            c["last"] = k
+            c["n"] += o["inc"]
+            place[k] = (c["sem"], c["n"])
+    assert used[0] <= NSEM, used[0]
+
+    for k, o in enumerate(ops):
+        if o["fixed"] is not None:
+            continue
+        q = queues[o["q"]]
+        best = {}
+        for j in o["waits"]:
+            s, v = place[j]
+            best[s] = max(v, best.get(s, 0))
+        for s in sorted(best):
+            q.wait_ge(T.sem[s], best[s])
+        if o["f"] is None:
+            continue
+        x = o["f"]()
+        if k in place:
+            x.then_inc(T.sem[place[k][0]], o["inc"])
+    g.wait_ge(T.sem["sent"], sent[0])

@@ -9,33 +9,33 @@ F, BFT, I32, U16, F16 = "float32", "bfloat16", "int32", "uint16", "float16"
 NDUMP = 640
 SCRATCH = {}
 for _n, _c, _t in [
-        ("i1", 128, I32), ("i1b", 128, I32), ("i2", 8, I32), ("i2b", 8, I32), ("i4", 128, I32),
-        ("i4b", 128, I32), ("i5", 128, I32), ("ki", 32, I32), ("kk", 32, U16), ("dj", 32, F),
-        ("mk", 8, F), ("i16", 512, F), ("z", 144, F), ("z16", 144, F16), ("ident", 128, F), ("mbf", 128, F),
-        ("mbb", 128, BFT), ("e8", 128, F), ("n1", 128, F), ("n2", 128, F), ("p1", 128, F), ("p2", 128, F),
+        ("ia", 144, I32), ("iab", 128, I32), ("i2", 8, I32), ("i2b", 8, I32), ("i5", 128, I32), ("dj", 32, F),
+        ("mk", 8, F), ("nm", 8, F), ("i16", 128, F), ("ident", 128, F), ("e8", 128, F), ("e8b", 128, BFT),
+        ("idf", 8, F16), ("n1", 128, F16), ("zb", 144, BFT), ("zc", 144, BFT), ("pos", 512, BFT),
         ("repb", 1024, BFT), ("repf", 1024, F),
-        ("tf", 2048, BFT), ("far", 2048, BFT), ("v8", 512, F), ("v16", 512, F), ("xi", 128, I32), ("ln", 32, I32),
-        ("laf", 16, F), ("lau", 16, U16), ("lbu", 16, U16), ("lu", 32, U16), ("lf", 128, U16),
-        ("xu", 64, U16), ("obu", 32, U16), ("xpa", 34, F), ("xpb", 34, F),
-        ("r1", 16, I32), ("r2", 16, I32), ("r3", 16, I32), ("r4", 16, I32), ("r5", 16, I32), ("r6", 16, I32),
-        ("ea", 32, F), ("ca", 32, F), ("da", 32, F), ("fma", 32, F), ("ga", 32, F), ("offa", 32, U16),
-        ("eb", 32, F), ("cb2", 32, F), ("db", 32, F), ("fmb", 32, F), ("gb", 32, F), ("offb", 32, U16),
-        ("exa", 512, BFT), ("exb", 512, BFT),
-        ("pk0", 32, F), ("pk", 32, F), ("exp", 512, F), ("fp", 512, F), ("pm", 512, F), ("pm2", 256, F),
-        ("pm4", 128, F), ("pm8", 64, F), ("pint", 32, I32),
-        ("xao", 32, I32), ("xbo", 32, I32), ("u1", 32, I32), ("u2", 32, I32), ("u3", 32, I32), ("u4", 32, I32),
-        ("u5", 32, I32), ("u6", 32, I32), ("xaou", 32, U16),
+        ("tf", 2048, BFT), ("far", 2048, BFT), ("v8", 512, F), ("v16", 512, F), ("xi", 128, I32), ("ll", 32, I32),
+        ("llh", 32, F16), ("lau", 16, U16), ("lu", 32, U16), ("lf", 128, U16), ("xu", 96, U16),
+        ("r1", 32, I32), ("r2", 32, I32), ("r3", 32, I32), ("r4", 32, I32), ("r5", 32, I32), ("pli", 32, I32),
+        ("pla", 16, U16), ("kl", 16, I32), ("ml", 16, F), ("nl", 16, F), ("offl", 16, U16),
+        ("ka", 64, I32), ("ma", 64, F), ("na", 64, F), ("sa", 64, I32),
+        ("ko", 32, I32), ("mo", 32, F), ("no", 32, F), ("obt", 32, U16),
+        ("xa16", 32, F16), ("nea", 32, BFT), ("ga", 32, F), ("offa", 32, U16), ("rowa", 512, BFT),
+        ("xb16", 32, F16), ("neb", 32, BFT), ("gb", 32, F), ("offb", 32, U16), ("rowb", 512, BFT),
+        ("wina", 2048 + NDUMP, BFT), ("winb", 2048 + NDUMP, BFT), ("winc", 2048, BFT), ("winl", 2048, BFT),
+        ("met", 2048, BFT), ("lista", 128, BFT), ("listb", 128, BFT), ("listc", 128, BFT), ("listl", 128, BFT),
+        ("enda", 128, U16), ("endb", 128, U16), ("lcomp", 128, U16), ("linv", 128, U16),
+        ("xr", 512, I32), ("gx", 512, F16), ("pk", 32, I32), ("xbo", 32, I32), ("xao", 32, I32), ("xaou", 32, U16),
         ("s1", 512, BFT), ("land1", 512, BFT), ("tb", 2048, BFT), ("tc", 2048, BFT), ("vc", 512, F), ("vcp", 512, F),
-        ("wa", 512, F), ("ra", 512, F), ("w1", 2048 + NDUMP, F), ("s3", 224, F), ("q3", 256, F), ("fan", 256, F),
-        ("w2", 2048, F), ("gt", 2048, F), ("ya1", 256, F), ("ya2", 256, F),
-        ("s5", 224, F), ("land3", 256, F), ("land5", 256, F), ("land6", 256, F), ("ta", 2048, F), ("wb", 512, F),
-        ("rb", 512, F), ("w3", 2048 + NDUMP, F), ("s6", 224, F), ("q6", 256, F), ("w4", 2048, F), ("yb2", 256, F)]:
+        ("wa", 512, F), ("ra", 520, F), ("s3", 256, F), ("q3", 264, F), ("fan", 256, F),
+        ("w2", 2048, F), ("gt", 2048, F), ("ya2", 256, F),
+        ("s5", 256, F), ("s5x", 512, F), ("land3", 256, F), ("land5", 256, F), ("land6", 256, F),
+        ("ta", 2048, F), ("wb", 512, F), ("rb", 520, F), ("s6", 256, F), ("q6", 264, F), ("yb2", 256, F)]:
     SCRATCH[_n] = ("sbuf", [128, _c], _t)
-SCRATCH["ll"] = ("sbuf", [128, 8, 4], I32)
-SCRATCH["rr"] = ("sbuf", [128, 8, 8, 4], F16)
-SCRATCH["rra"] = ("sbuf", [128, 128], F)
+SCRATCH["l8"] = ("sbuf", [128, 2, 16, 16], I32)
+SCRATCH["l8h"] = ("sbuf", [128, 2, 16, 16], F16)
+SCRATCH["idh"] = ("sbuf", [128, 8, 16], BFT)
 for _k in range(8):
-    SCRATCH["ps%d" % _k] = ("psum", [128, 512], F)
+    SCRATCH["ps%d" % _k] = ("psum", [128, 512] if _k in (1, 5, 6) else [128, 2, 256], F)
 NSEM = 130
 SEMAPHORES = ["e%d" % k for k in range(NSEM)] + ["arr%d%s" % (k, s) for k in (1, 3, 5, 6) for s in "fhsn"] + ["sent"]
 
@@ -80,11 +80,19 @@ def rank_program(g, core, T, topo):
         return k
 
     def A(n, lo=0, hi=None, p0=0, p1=128, step=1):
+        if n[:2] == "ps" and len(SCRATCH[n][1]) == 3:
+            hi = 512 if hi is None else hi
+            h = lo // 256
+            ap = T[n][p0:p1, h, lo - 256 * h:hi - 256 * h:step] if hi <= 256 * h + 256 else T[n][p0:p1, :, lo:256:step]
+            return (ap, [(n, p0, p1, lo, hi)])
         hi = SCRATCH[n][1][1] if hi is None else hi
         return (T[n][p0:p1, lo:hi] if step == 1 else T[n][p0:p1, lo:hi:step], [(n, p0, p1, lo, hi)])
 
     def X(ap, n, lo, hi):
         return (ap, [(n, 0, 128, lo, hi)])
+
+    def rows(n, lo, hi, p0=0):
+        return (T[n][p0:128:16, lo:hi], [(n, 0, 128, lo, hi)])
 
     def ind(win, off):
         return (win[0].indirect(off[0]), win[1] + off[1])
@@ -97,6 +105,10 @@ def rank_program(g, core, T, topo):
 
     def scaled(out, in_, s, grp=None):
         record("s", lambda: g.scalar.activation(out[0], in_[0], COPY, scale=s[0]), [out], [in_, s], grp)
+
+    def constant(out, in_, c):
+        record("s", lambda: g.scalar.activation(out[0], in_[0], ActivationFunctionType.Identity, bias=c, scale=0.0),
+               [out], [in_])
 
     def tt(out, a, b, o, grp=None):
         record("v", lambda: g.vector.tensor_tensor(out[0], a[0], b[0], o), [out], [a, b], grp)
@@ -119,16 +131,12 @@ def rank_program(g, core, T, topo):
     def mm(out, l, r, start, stop, grp):
         record("t", lambda: g.tensor.matmul(out[0], l[0], r[0], start, stop), [out], [l, r], grp)
 
-    def iota(n, cols, pattern, base, cm, fl=False):
-        out = A(n, 0, cols)
-        if fl:
+    def iota(n, pattern, base, cm, lo=0):
+        out = A(n, lo)
+        if SCRATCH[n][2] != I32:
             record("g", lambda: g.iota(out[0], pattern, base, cm, allow_small_or_imprecise_dtypes=True), [out], [])
         else:
             record("g", lambda: g.iota(out[0], pattern, base, cm), [out], [])
-
-    def pick(n, base):
-        out, same = A(n), A("mbf")
-        record("g", lambda: g.affine_select(out[0], same[0], [[-1, 128]], OPS.is_equal, 0.0, base, 1), [out], [same])
 
     def scan(out, keep, x):
         record("v", lambda: g.vector.tensor_tensor_scan(out[0], keep[0], x[0], 0.0, OPS.mult, OPS.add), [out], [keep, x])
@@ -153,7 +161,6 @@ def rank_program(g, core, T, topo):
     others = [q for q in ranks if q != me and q not in sib and q not in near]
     far0 = [q for q in others if row(q) == row(me)]
     far1 = [q for q in others if q not in far0]
-    order = far0 + far1 + sib + near + [me]
     p_own, p_far0, p_far1, p_near = min(sib + [me]), min(far0), min(far1), min(near)
     kinds = (("s", sib), ("f", far0), ("h", far1), ("n", near))
 
@@ -170,268 +177,326 @@ def rank_program(g, core, T, topo):
 
     sent = [0]
 
-    def send(src, width, dst, arr, calls):
-        for dests in calls:
-            tr, rd = [], []
-            for q in dests:
-                d = order.index(q)
-                s = A(src, d * width, (d + 1) * width)
-                rd.append(s)
-                rid, pid = topo.addr(cores[q])[:2]
-                es = engines_for(q, dests)
-                sent[0] += len(es)
-                w = [k for k, qs in kinds if q in qs][0]
-                tr.append(RemoteDMATransfer(dst_ids=[DstId(rid=rid, pnc=pid)], dma_engine_mask=sum(1 << e for e in es),
-                                            remote_sem=T.sem[arr + w], srcs=[s[0]],
-                                            dsts=[T[dst][:, width * me:width * me + width]]))
-            record("g", lambda tr=tr: g.remote_dma_fused(tr, local_sem=T.sem["sent"]), [], rd)
+    def send(src, width, dst, arr, dests):
+        tr, rd = [], []
+        for q in dests:
+            lo = q * width % SCRATCH[src][1][1]
+            s = A(src, lo, lo + width)
+            rd.append(s)
+            rid, pid = topo.addr(cores[q])[:2]
+            es = engines_for(q, dests)
+            sent[0] += len(es)
+            w = [k for k, qs in kinds if q in qs][0]
+            tr.append(RemoteDMATransfer(dst_ids=[DstId(rid=rid, pnc=pid)], dma_engine_mask=sum(1 << e for e in es),
+                                        remote_sem=T.sem[arr + w], srcs=[s[0]],
+                                        dsts=[T[dst][:, width * me:width * me + width]]))
+        record("g", lambda: g.remote_dma_fused(tr, local_sem=T.sem["sent"]), [], rd)
 
-    def arrival(n, width, arr, calls):
+    def arrival(n, width, arr, calls, own=None):
         for w, srcs in kinds:
-            regs = [(n, 0, 128, q * width, (q + 1) * width) for q in srcs]
+            m, c = own if own and srcs is sib else (n, width)
+            regs = [(m, 0, 128, q * c, (q + 1) * c) for q in srcs]
             num = sum(len(engines_for(q, dests)) for dests in calls for q in dests if q in srcs)
             record("in_" + arr + w, None, [(None, regs)], [], fixed=(arr + w, num))
 
-    calls1 = (far0 + far1, near + sib)
-    calls3 = (far0, far1, near + sib)
-    calls5 = (far0, far1 + sib, near)
+    calls1 = (sib, far0, far1, near)
+    calls3 = (far0, far1, near, sib)
 
-    dma("y", X(T["ll"][:, 0:4, :], "ll", 0, 16), ext(T["lb"][:, :], "lb"), "d_l")
-    dma("s", X(T["ll"][:, 4:8, :], "ll", 16, 32), ext(T["lc"][:, :], "lc"), "d_l")
+    for k, n in enumerate(("lc", "lb")):
+        dma("ys"[k], X(T["l8"][0:8, k, :, :], "l8", k, k + 1), ext(T[n][:, :], n), "d_l")
+    dma("s", A("v8", 0, 512, 0, 8), ext(T["v"][:, :], "v"), None)
     for k in range(8):
-        n = "fb" if k < 4 else "fc"
+        n = "fb" if k % 2 else "fc"
         dma("ys"[k % 2], A("tf", 0, 2048, 16 * k, 16 * k + 16), ext(T[n][:, :], n), "d_tf")
-    for k, n in enumerate(("xa", "xb", "xc", "ob")):
+    for k, n in enumerate(("xa", "xb")):
+        dma("ys"[k], A("xi", 32 * k, 32 * k + 32), ext(T[n][:, :], n), None)
+    dma("y", A("ll", 16, 32), ext(T["la"][:, :], "la"), None)
+    for k, n in ((2, "xc"), (3, "ob")):
         dma("y", A("xi", 32 * k, 32 * k + 32), ext(T[n][:, :], n), "d_x")
-    dma("y", A("v8", 0, 512, 0, 8), ext(T["v"][:, :], "v"), "d_x")
-    dma("y", A("ln", 0, 16), ext(T["la"][:, :], "la"), "d_x")
-    dma("y", A("ln", 16, 32), ext(T["lb"][:, :], "lb"), "d_x")
 
-    iota("i2", 8, [[-16, 8]], 0, 1)
-    iota("i1", 128, [[0, 8], [-1, 16]], 16, 1)
-    iota("i4", 128, [[-16, 8], [0, 16]], 0, 1)
-    iota("i5", 128, [[1, 8], [0, 16]], 0, -1)
-    iota("dj", 32, [[16, 32]], 2048, 1, True)
-    iota("ki", 32, [[1, 32]], 0, 0)
-    fill(A("z"), 0.0)
+    iota("ia", [[1, 144]], 0, -1)
+    iota("i2", [[-16, 8]], 0, 1)
+    iota("i5", [[1, 8], [0, 16]], 0, -1)
+    iota("dj", [[16, 32]], 2048, 1)
+    iota("pos", [[1, 512]], -256, 0)
+    fill(A("winc", 0, 768), 256.0)
+    for s in "abl":
+        dma("y", rows("win" + s, 0, 2048), A("winc", 0, 512, 0, 32), None)
+    ts(A("iab"), A("ia", 0, 128), 15, OPS.bitwise_and)
     ts(A("i2b"), A("i2"), 4, OPS.arith_shift_right)
+    ts(A("i16"), A("iab"), 0, OPS.is_equal)
     ts(A("mk"), A("i2b"), 0, OPS.is_equal)
-    ts(A("i1b"), A("i1"), 15, OPS.bitwise_and)
-    ts(A("i16", 0, 128), A("i1b"), 0, OPS.is_equal)
-    cp("v", A("z", 112, 128), A("i16", 0, 16))
-    ts(A("i4b"), A("i4"), 4, OPS.arith_shift_right)
-    cp("v", A("z16"), A("z"))
-    ts(A("mbf"), A("i4b"), 0, OPS.is_equal)
-    for n, k in (("n1", -1), ("n2", 15), ("p1", 1), ("p2", -15)):
-        pick(n, k)
-    for h in range(8):
-        scaled(A("repb", 128 * h, 128 * h + 128), A("i16", 0, 128), A("mk", h, h + 1), "g_repb")
-
-    for d in range(8):
-        r = order[d]
-        ts(X(T["rr"][:, :, d, :], "rr", d, d + 1), X(T["ll"][:, :, :], "ll", 0, 32), A("mk", r, r + 1), OPS.mult,
-           grp="g_rr")
-    for h in range(8):
-        b = 32 * (h // 2)
-        mm((T["ps4"][b:b + 32, 0:32], [("ps4", b, b + 32, 0, 32)]), A("z16", 112 - 16 * (h % 2), 144 - 16 * (h % 2)),
-           X(T["rr"][:, h, :, :], "rr", 0, 8), h % 2 == 0, h % 2 == 1, "g_lt")
-    fill(A("xpa"), -1.0)
-    cp("v", A("mbb"), A("mbf"))
-    cp("v", A("lu"), A("ps4", 0, 32))
-    fill(A("xpb"), -1.0)
-    cp("v", A("kk"), A("ki"))
+    ts(X(T["idh"][:, :, :], "idh", 0, 128), A("ia", 0, 128), 0, OPS.is_equal)
     ts(A("e8"), A("i5"), 0, OPS.is_equal)
-    cp("v", A("s1", 0, 256), ind(A("tf"), A("lu", 0, 16)))
-    cp("s", A("s1", 256, 512), ind(A("tf"), A("lu", 16, 32)))
-    send("s1", 64, "land1", "arr1", calls1)
-    pick("ident", 0)
-    iota("w1", 2048, [[0, 2048]], 0, 0, True)
-    rep, zero = A("repf"), A("w1", 0, 1024)
-    record("g", lambda: g.affine_select(rep[0], zero[0], [[-16, 8], [0, 8], [-1, 16]], OPS.not_equal, 1.0, 0, 1),
-           [rep], [zero])
-    iota("w2", 2048, [[0, 2048]], 0, 0, True)
-    cp("s", A("land1", 64 * me, 64 * me + 64), A("s1", 448, 512))
+    for h in range(8):
+        scaled(A("repb", 128 * h, 128 * h + 128), A("i16"), A("mk", h, h + 1), "g_repb")
 
-    for k in range(1, 4):
-        cp("s", A("i16", 128 * k, 128 * k + 128), A("i16", 0, 128), "g_i16")
-    cp("v", A("xpa", 1, 33), A("xi", 0, 32))
-
-    def shift(xp, ps, s):
-        mm(A(ps, 0, 32), A("n1"), A(xp, 1, 33), True, False, "g_n" + s)
-        mm(A(ps, 0, 32), A("n2"), A(xp, 2, 34), False, True, "g_n" + s)
-        mm(A(ps, 32, 64), A("p1"), A(xp, 1, 33), True, False, "g_n" + s)
-        mm(A(ps, 32, 64), A("p2"), A(xp, 0, 32), False, True, "g_n" + s)
-
-    def ends(xp, ps, s, off):
-        tt(A("e" + s), A(ps, 0, 32), A(xp, 1, 33), OPS.not_equal)
-        tt(A("fm" + s), A("d" + s), A("e" + s), OPS.mult)
-        tt(A("g" + s), A("fm" + s), A("dj"), OPS.add)
-        cp("v", A(off), A("g" + s))
-
-    def spread(out, x, grp):
-        for i in range(16):
-            scaled(A(out, i, 512, step=16), A(x), A("i16", i, i + 1), grp)
-
-    shift("xpa", "ps7", "a")
+    ts(A("nm", 0, 1), A("i16", 0, 1), 0, OPS.is_equal)
+    ts(A("zb"), A("ia"), 15, OPS.is_equal, A("i16", 0, 1), OPS.mult)
+    ts(A("idf"), A("ia", 0, 8), 0, OPS.is_equal)
+    cp("v", X(T["l8h"][0:8, :, :, :], "l8h", 0, 2), X(T["l8"][0:8, :, :, :], "l8", 0, 2))
+    for k in range(16):
+        mm(A("ps4", k % 4, 32, 32 * (k // 4), 32 * (k // 4) + 32, 4), X(T["l8h"][0:8, :, :, k], "l8h", 0, 2),
+           A("idf", 0, 8, 0, 8), True, True, "g_lt")
     mm(A("ps5"), A("e8", 0, 128, 0, 8), A("v8", 0, 512, 0, 8), True, True, "g_v")
-    ts(A("pk0"), A("xi", 32, 64), 2048, OPS.mult)
-    tt(A("da"), A("xpa", 1, 33), A("dj"), OPS.subtract)
-    tt(A("ca"), A("ps7", 32, 64), A("xpa", 1, 33), OPS.is_equal)
-    cp("s", A("v16"), A("ps5"))
-    ends("xpa", "ps7", "a", "offa")
-    cp("v", A("xu"), A("xi", 32, 96))
-    tt(A("exa"), ind(A("ca"), A("kk")), A("i16"), OPS.mult)
-    tt(A("pk"), A("pk0"), A("xpa", 1, 33), OPS.add)
-    cp("v", A("obu"), A("xi", 96, 128))
-    cp("v", A("lau"), A("ln", 0, 16))
-    cp("v", A("laf"), A("ln", 0, 16))
+    ts(A("n1"), A("ia", 0, 128), -1, OPS.is_equal, A("nm", 0, 1), OPS.mult)
+    cp("v", A("lu"), A("ps4", 0, 32))
+    cp("s", A("e8b"), A("e8"))
+    ts(A("nm", 1, 2), A("i16", 1, 2), 2048, OPS.mult, A("i16", 0, 1), OPS.add)
+    ts(A("nm", 2, 3), A("i16", 1, 2), -1, OPS.mult, 15, OPS.add)
+    ts(A("zc"), A("ia"), A("nm", 2, 3), OPS.is_equal, A("nm", 1, 2), OPS.mult)
+    for e, p in (("v", p_far0), ("s", p_own), ("v", p_far1), ("s", p_near)):
+        cp(e, A("s1", 64 * p, 64 * p + 128), ind(A("tf"), A("lu", 4 * p, 4 * p + 8)))
+    for dests in calls1:
+        send("s1", 64, "land1", "arr1", dests)
+    cp("s", A("land1", 64 * me, 64 * me + 64), A("s1", 64 * me, 64 * me + 64))
+    iota("xr", [[0, 512]], 0, 0)
+    for n, lo in (("ra", 512), ("rb", 512), ("q3", 256), ("q6", 256)):
+        iota(n, [[0, 8]], 0, 0, lo)
+    iota("w2", [[0, 2048]], 0, 0)
 
-    arrival("land1", 64, "arr1", calls1)
-    for k in range(8):
-        dma("y", A("far", 0, 2048, 16 * k, 16 * k + 16), ext(T["fa"][:, :], "fa"), "d_fa",
-            [A("land1", 64 * q, 64 * q + 64) for q in near])
-    for f, q, n, k, e in ((1, p_own, 2, 0, "s"), (0, p_own, 2, 4, "v"), (1, p_far0, 2, 1, "s"),
-                          (1, p_far1, 2, 2, "v"), (0, p_far0, 2, 5, "s"), (0, p_far1, 2, 6, "v"),
-                          (1, p_near, 1, 3, "s"), (1, p_near + 1, 1, 0, "v"), (0, p_near, 2, 7, "s")):
+    def following(x, ps, s):
+        mm(A(ps, 0, 32), A("n1"), A(x, 0, 32), True, False, "g_n" + s)
+        mm(A(ps, 0, 31), A("zb", 0, 128), A(x, 1, 32), False, True, "g_n" + s)
+
+    def by_rows(x, s, out, n=128):
+        ts(A("k" + s), x, 4, OPS.arith_shift_right)
+        ts(A("m" + s), x, n, OPS.mult)
+        ts(A("n" + s), A("k" + s), 1 - 16 * n, OPS.mult)
+        tt(A(out), A("m" + s), A("n" + s), OPS.add)
+
+    def ends(x, place, ps, s):
+        tt(A("ne" + s), A(ps, 0, 32), A(x), OPS.is_equal)
+        tt(A("g" + s), A("dj"), A("ne" + s), OPS.mult)
+        dma("y", A("row" + s, 0, 512, 0, 8), A("ne" + s), None)
+        tt(A("off" + s), A("g" + s), place, OPS.max)
+
+    def invert(s, lo=0):
+        cp("v", ind(A("win" + s), A("off" + s)), A("pos", lo, 512))
+        dma("y", A("list" + s), rows("win" + s, 0, 2048), None)
+
+    def keep(ps, s):
+        for i in range(16):
+            lo = 32 * (i - 1) if i else 479
+            mm(A(ps, i, 512, step=16), A("e8b", 0, 128, 0, 8), A("row" + s, lo, lo + 32, 0, 8), True, True, "g_k" + s)
+
+    def table(f, q, n, k, e):
         for i in range(4 * n):
-            w = 128 * (4 * f + i % 4)
+            w = 128 * (2 * (i % 4) + f)
             lo = 64 * (q + i // 4)
             mm(A("ps%d" % k, 64 * i, 64 * i + 64), A("repb", w, w + 128), A("land1", lo, lo + 64), True, True,
-               "g_t%d%d" % (k, q))
-        cp(e, A("tb" if f == 0 else "tc", 256 * q, 256 * (q + n)), A("ps%d" % k, 0, 256 * n))
-    mm(A("ps1"), A("mbb"), A("exa"), True, True, "g_ma")
+               "g_t%d%d%d" % (f, k, q))
+        cp(e, A("tb" if f else "tc", 256 * q, 256 * (q + n)), A("ps%d" % k, 0, 256 * n))
+
+    ts(A("xa16"), A("xi", 0, 32), 1, OPS.add)
+    following("xa16", "ps7", "a")
+    by_rows(A("xi", 0, 64), "a", "sa")
+    ends("xa16", A("sa", 0, 32), "ps7", "a")
+    for k in range(2):
+        cp("v", A("llh", 16 * k, 16 * k + 16), A("ll", 16, 32), "g_lah")
+    invert("a")
+    constant(A("winc", 768, 2048), A("tf", 768, 2048), 256.0)
+    table(0, me, 1, 0, "s")
+    table(1, me, 1, 4, "s")
+    cp("s", A("v16"), A("ps5"))
+    cp("s", A("ident"), X(T["idh"][:, :, :], "idh", 0, 128))
+    cp("s", A("repf", 0, 512), A("repb", 0, 512))
+    cp("v", A("lau"), A("ll", 16, 32))
+    chips5 = (p_far0, p_far1, p_near, p_own)
+    parts = ((0, 5), (5, 8))
+    for lo, hi in parts:
+        for d in range(lo, hi):
+            r = chips5[d // 2] + d % 2
+            for a in range(4):
+                mm(A("ps6", 16 * lo + d - lo, 16 * hi, 32 * a, 32 * a + 32, hi - lo), A("llh"),
+                   X(T["idh"][:, r, :], "idh", 0, 128), True, True, "g_lf")
+    cp("v", ind(A("winc"), A("lau")), A("pos", 256, 512))
+    cp("v", A("lf"), A("ps6", 0, 128))
+    cp("v", A("xu"), A("xi", 32, 128))
+    by_rows(A("xi", 96, 128), "o", "obt", 32)
+
+    arrival("land1", 64, "arr1", calls1)
+    through = [A("land1", 64 * q, 64 * q + 64) for q in near]
+    dma("y", rows("xr", 0, 512), ext(T["xa"][:, :], "xa"), "d_xr", through)
+    dma("y", rows("xr", 0, 512, 1), A("sa", 32, 64), "d_xr", through)
+    dma("y", A("ll", 0, 16), ext(T["lb"][:, :], "lb"), None, through)
+    for k in range(8):
+        dma("y", A("far", 0, 2048, 16 * k, 16 * k + 16), ext(T["fa"][:, :], "fa"), "d_fa", through)
+    table(0, sib[0], 1, 0, "s")
+    table(1, sib[0], 1, 4, "s")
+    table(0, p_far0, 2, 1, "v")
+    table(1, p_far0, 2, 5, "s")
+    table(0, p_far1, 2, 2, "v")
+    table(1, p_far1, 2, 6, "s")
+    table(0, p_near, 1, 3, "v")
+    table(0, p_near + 1, 1, 0, "s")
+    table(1, p_near, 2, 7, "s")
+    keep("ps1", "a")
     tt(A("vc"), ind(A("tc"), A("xu", 32, 64)), A("v16"), OPS.mult)
+
+    def meet(d):
+        lo, hi = parts[d]
+        cp("s", A("met", 256 * lo, 256 * hi), ind(A("winc"), A("lf", 16 * lo, 16 * hi)))
+        dma("y", A("listc", 16 * lo, 16 * hi), rows("met", 256 * lo, 256 * hi), None)
+
+    def meet_list(d):
+        lo, hi = parts[d]
+        cp("v", A("lcomp", 16 * lo, 16 * hi), A("listc", 16 * lo, 16 * hi))
+
+    meet(0)
     tt(A("wa"), ind(A("tb"), A("xu", 0, 32)), A("vc"), OPS.mult)
-    scan(A("ra"), A("ps1"), A("wa"))
-    cp("v", ind(A("w1"), A("offa")), A("ra"))
-    spread("exp", "pk", "g_exp")
-    mm(A("ps2"), A("mbf"), A("exp"), True, True, "g_fp")
-    cp("s", A("fp"), A("ps2"))
-    cp("s", A("vcp"), ind(A("vc"), A("obu")))
+    ts(A("enda"), A("lista"), 256, OPS.add)
+    scan(A("ra", 0, 512), A("ps1"), A("wa"))
 
-    def add_slabs(w, s, land, arr):
-        for qs, k in ((far0, 0), (far1, 1), (near + sib, 2), ([me], 3)):
-            for q in qs:
-                for b in range(2):
-                    c = 32 * (order.index(q) % 4)
-                    mm(A("ps%d" % k, c + b, c + 32, step=2), A(w, 256 * q + 128 * b, 256 * q + 128 * b + 128),
-                       A("i16", 0, 16), True, True, "g_%s%d" % (w, k))
-        cp("v", A(s, 0, 64), A("ps0", 0, 64))
-        cp("v", A(s, 64, 128), A("ps1", 64, 128))
-        cp("s", A(s, 128, 224), A("ps2", 0, 96))
-        send(s, 32, land, arr, calls3)
-        cp("s", A(land, 32 * me, 32 * me + 32), A("ps3", 96, 128))
+    def add_groups(win, lst, col, out, e, grp):
+        cp(e, A("gt", col, col + 128 * len(out)), ind(A(win), A(lst[0], lst[1], lst[1] + 8 * len(out))))
+        for b, o in enumerate(out):
+            mm(o, A("gt", col + 128 * b, col + 128 * b + 128), A("i16", 0, 16), True, True, grp)
 
-    add_slabs("w1", "s3", "land3", "arr3")
-    iota("w3", 2048, [[0, 2048]], 0, 0, True)
+    def add_slabs(win, lst, s, land, arr):
+        def part(q, k, e, lo=0, hi=2):
+            c = 32 * (q % 2)
+            out = [A("ps%d" % k, c + b, c + 32, step=2) for b in range(lo, hi)]
+            add_groups(win, (lst, 16 * q + 8 * lo), 256 * q + 128 * lo, out, e, "g_%s%d%d" % (win, k, q == me))
+
+        def out(p, n, k, e, call):
+            cp(e, A(s, 32 * p, 32 * (p + n)), A("ps%d" % k, 32 * (p % 2), 32 * (p % 2 + n)))
+            send(s, 32, land, arr, calls3[call])
+
+        for b in range(2):
+            part(far0[0], 0, "v", b, b + 1)
+            part(far0[1], 0, "s", b, b + 1)
+        part(far1[0], 1, "v")
+        part(far1[1], 1, "s")
+        out(p_far0, 2, 0, "v", 0)
+        part(near[0], 2, "s")
+        part(near[1], 2, "v")
+        out(p_far1, 2, 1, "s", 1)
+        part(sib[0], 3, "v")
+        part(me, 0, "s")
+        out(p_near, 2, 2, "v", 2)
+        out(sib[0], 1, 3, "v", 3)
+        cp("s", A(land, 32 * me, 32 * me + 32), A("ps0", 32 * (me % 2), 32 * (me % 2) + 32))
+
+    add_slabs("ra", "enda", "s3", "land3", "arr3")
 
     cp("s", A("fan"), ind(A("far"), A("lau")))
-    for d in range(8):
-        r = order[d]
-        scaled(A("rra", 16 * d, 16 * d + 16), A("laf"), A("mk", r, r + 1), "g_rra")
-    mm(A("ps4", 0, 128), A("i16", 0, 128), A("rra"), True, True, "g_lf")
-    tt(A("pm"), ind(A("fp"), A("obu")), A("i16"), OPS.mult)
-    tt(A("pm2"), A("pm", 0, 512, step=2), A("pm", 1, 512, step=2), OPS.add)
-    cp("v", A("lf"), A("ps4", 0, 128))
-    tt(A("pm4"), A("pm2", 0, 256, step=2), A("pm2", 1, 256, step=2), OPS.add)
-    tt(A("pm8"), A("pm4", 0, 128, step=2), A("pm4", 1, 128, step=2), OPS.add)
-    tt(A("pint"), A("pm8", 0, 64, step=2), A("pm8", 1, 64, step=2), OPS.add)
-
-    def to_natural(land, q, pa, pb):
-        mm(A(pa, 0, 128), A(land, 0, 256, step=2), A("ident"), True, True, "g_n0" + land)
-        mm(A(pb, 0, 128), A(land, 1, 256, step=2), A("ident"), True, True, "g_n1" + land)
-        cp("s", A(q, 0, 128), A(pa, 0, 128))
-        cp("v", A(q, 128, 256), A(pb, 0, 128))
+    meet(1)
+    cp("s", A("repf", 512, 1024), A("repb", 512, 1024))
+    cp("v", A("gx"), ind(A("xr"), A("obt")))
+    for i in range(16):
+        mm(A("ps5", 0, 32), A("zc", 15 - i, 143 - i), A("gx", i, 512, step=16), i == 0, i == 15, "g_pk")
+    meet_list(0)
+    ts(A("r1"), A("ll"), 480, OPS.bitwise_and)
+    ts(A("r2"), A("ll"), 511, OPS.bitwise_and)
+    ts(A("r3"), A("ll"), 4, OPS.arith_shift_right, 96, OPS.bitwise_and)
+    ts(A("r4"), A("r1"), 3, OPS.mult)
+    tt(A("r5"), A("r2"), A("r3"), OPS.add)
+    tt(A("pli"), A("r5"), A("r4"), OPS.add)
+    cp("v", A("pk"), A("ps5", 0, 32))
+    ts(A("xbo"), A("pk"), 11, OPS.arith_shift_right)
+    ts(A("xao"), A("pk"), 2047, OPS.bitwise_and)
+    ts(A("xb16"), A("xbo"), 1, OPS.add)
 
     arrival("land3", 32, "arr3", calls3)
-    to_natural("land3", "q3", "ps6", "ps7")
-    tt(ind(A("w2"), A("lau")), A("q3"), A("fan"), OPS.mult)
-    bank = (0, 0, 1, 1, 1, 2, 2, 3)
-    for d in range(8):
-        for lo, hi in ((0, 128), (128, 256)) if d < 2 else ((0, 256),):
-            cp("vsvsvssv"[d], A("gt", 256 * d + lo, 256 * d + hi),
-               ind(A("w2"), A("lf", 16 * d + lo // 16, 16 * d + hi // 16)))
-        for b in range(2):
-            c = 32 * (d % 4) + 16 * b
-            mm(A("ps%d" % bank[d], c, c + 16), A("gt", 256 * d + 128 * b, 256 * d + 128 * b + 128), A("i16", 0, 16),
-               True, True, "g_m%d" % bank[d])
-        if d == 2:
-            turn(A("s5", 0, 64), A("ps0", 0, 64))
-    turn(A("s5", 64, 128), A("ps1", 64, 128))
-    turn(A("s5", 128, 160), A("ps1", 0, 32))
-    turn(A("s5", 160, 224), A("ps2", 32, 96))
-    turn(A("land5", 32 * me, 32 * me + 32), A("ps3", 96, 128))
-    send("s5", 32, "land5", "arr5", calls5)
-    iota("w4", 2048, [[0, 2048]], 0, 0, True)
+    for b in range(2):
+        mm(A("ps%d" % (6 + b), 0, 128), A("land3", b, 256, step=2), A("ident"), True, True, None)
+        tt(A("q3", 128 * b, 128 * b + 128), A("ps%d" % (6 + b), 0, 128), A("fan", 128 * b, 128 * b + 128), OPS.mult)
+    following("xb16", "ps5", "b")
 
-    ts(A("xbo"), A("pint"), 11, OPS.arith_shift_right)
-    cp("v", A("xpb", 1, 33), A("xbo"))
-    shift("xpb", "ps1", "b")
-    ts(A("xao"), A("pint"), 2047, OPS.bitwise_and)
-    tt(A("db"), A("xpb", 1, 33), A("dj"), OPS.subtract)
-    tt(A("cb2"), A("ps1", 32, 64), A("xpb", 1, 33), OPS.is_equal)
-    spread("exb", "cb2", "g_exb")
-    ends("xpb", "ps1", "b", "offb")
-    ts(A("u1"), A("xao"), 5, OPS.arith_shift_right, 7, OPS.bitwise_and)
-    ts(A("u2"), A("xao"), 8, OPS.arith_shift_right, 1, OPS.bitwise_and)
-    ts(A("u3"), A("u1"), 32, OPS.mult)
-    ts(A("u4"), A("u2"), -224, OPS.mult)
-    tt(A("u5"), A("u3"), A("xao"), OPS.add)
-    tt(A("u6"), A("u4"), A("u5"), OPS.add)
-    cp("v", A("xaou"), A("u6"))
+    def part5(q, k, e, halves=False):
+        c = 32 * (q % 2)
+        out = [A("ps%d" % k, c + 16 * b, c + 16 * b + 16) for b in range(2)]
+        for lo, hi in ((0, 1), (1, 2)) if halves else ((0, 2),):
+            add_groups("q3", ("lcomp", 32 * chips5.index(q - q % 2) + 16 * (q % 2) + 8 * lo), 256 * q + 128 * lo,
+                       out[lo:hi], e[lo], "g_m%d" % k)
 
-    arrival("land5", 32, "arr5", calls5)
-    for q, k, u0, u1, e in ((p_far0, 5, 0, 8, "v"), (p_own, 4, 0, 8, "s"), (p_far1, 6, 0, 8, "v"),
-                            (p_near, 7, 0, 4, "s"), (p_near, 3, 4, 6, "v"), (p_near, 0, 6, 8, "s")):
+    def out5(p, n, k, call):
+        turn(A("s5", 32 * p, 32 * (p + n)), A("ps%d" % k, 32 * (p % 2), 32 * (p % 2 + n)))
+        send("s5", 32, "land5", "arr5", calls3[call])
+
+    def whole(q, k, e, out):
+        d = 6 + q % 2
+        cp(e, A("gt", 256 * q, 256 * q + 256), ind(A("q3"), A("lcomp", 16 * d, 16 * d + 16)))
+        mm(A("ps%d" % k, 0, 256), A("i16"), A("gt", 256 * q, 256 * q + 256), True, True, None)
+        cp("s", out, A("ps%d" % k, 0, 256))
+
+    part5(far0[0], 0, "vs", True)
+    part5(far0[1], 0, "vs", True)
+    part5(far1[0], 1, "v")
+    part5(far1[1], 1, "s")
+    out5(p_far0, 2, 0, 0)
+    meet_list(1)
+    part5(near[0], 2, "s")
+    part5(near[1], 2, "v")
+    out5(p_far1, 2, 1, 1)
+    whole(sib[0], 3, "s", A("s5x", 256 * (sib[0] % 2), 256 * (sib[0] % 2) + 256))
+    out5(p_near, 2, 2, 2)
+    send("s5x", 256, "ta", "arr5", sib)
+    whole(me, 4, "v", A("ta", 256 * me, 256 * me + 256))
+
+    ends("xb16", A("xbo"), "ps5", "b")
+    invert("b")
+    cp("v", A("pla"), A("pli", 16, 32))
+    cp("v", A("xaou"), A("xao"))
+    by_rows(A("pli", 0, 16), "l", "offl")
+    cp("v", ind(A("w2"), A("pla")), A("q3", 0, 256))
+
+    arrival("land5", 32, "arr5", calls3, ("ta", 256))
+    cp("s", A("vcp"), ind(A("vc"), A("xu", 64, 96)))
+    for q, k, u0, u1, e in ((p_far0, 7, 0, 8, "s"), (p_far1, 0, 0, 8, "s"),
+                            (p_near, 4, 0, 4, "s"), (p_near, 3, 4, 6, "v"), (p_near, 2, 6, 8, "v")):
         for u in range(u0, u1):
             h = 2 * (u % 4) + u // 4
-            mm(A("ps%d" % k, 64 * (u - u0), 64 * (u - u0) + 64), A("repf", 128 * h, 128 * h + 128),
+            mm(X(T["ps%d" % k][:, :, 32 * u:32 * u + 32], "ps%d" % k, 0, 512), A("repf", 128 * h, 128 * h + 128),
                A("land5", 32 * q, 32 * q + 64), True, True, "g_u%d" % k)
-        cp(e, A("ta", 256 * q + 64 * u0, 256 * q + 64 * u1), A("ps%d" % k, 0, 64 * (u1 - u0)))
-    mm(A("ps2"), A("mbb"), A("exb"), True, True, "g_mb")
+        if u1 - u0 == 8:
+            cp(e, A("ta", 256 * q, 256 * q + 512), A("ps%d" % k))
+        else:
+            for w in range(2):
+                lo, hi = 256 * w + 32 * u0, 256 * w + 32 * u1
+                cp(e, A("ta", 256 * q + lo, 256 * q + hi), A("ps%d" % k, lo, hi))
+        if k == 0:
+            ts(A("endb"), A("listb"), 256, OPS.add)
+    keep("ps5", "b")
 
-    def sum_a(half, ps):
-        for k in range(8):
-            lo = 1024 * half + 128 * k
-            mm(A(ps, k, 128, step=8), A("w2", lo, lo + 128), A("i16", 0, 16), True, True, "g_ya%d" % half)
+    def new_a(half):
+        for j in range(4):
+            for e in range(2):
+                lo = 128 * (8 * e + 4 * half + j)
+                mm(A("ps%d" % (6 + half), 32 * j + e, 32 * j + 32, step=2), A("w2", lo, lo + 128), A("i16", 0, 16),
+                   True, True, "g_ya%d" % half)
 
-    sum_a(0, "ps4")
+    def store(n, s, banks):
+        for k in range(2):
+            turn(A(s, 128 * k, 128 * k + 128), A("ps%d" % banks[k], 0, 128))
+        for a in range(4):
+            dma("ys"[a % 2] if n == "yb" else "y", ext(T[n][:, 512 * a:512 * a + 512], "%s%d" % (n, a)),
+                A(s, 0, 256, 32 * a, 32 * a + 32), "d_" + n)
+
+    new_a(0)
     tt(A("wb"), ind(A("ta"), A("xaou")), A("vcp"), OPS.mult)
-    scan(A("rb"), A("ps2"), A("wb"))
-    cp("v", ind(A("w3"), A("offb")), A("rb"))
-    cp("s", A("ya1", 0, 128), A("ps4", 0, 128))
+    scan(A("rb", 0, 512), A("ps5"), A("wb"))
 
-    add_slabs("w3", "s6", "land6", "arr6")
+    add_slabs("rb", "endb", "s6", "land6", "arr6")
 
-    sum_a(1, "ps5")
-    cp("s", A("ya1", 128, 256), A("ps5", 0, 128))
-    for k in range(2):
-        mm(A("ps%d" % (6 + k), 0, 128), A("ya1", 128 * k, 128 * k + 128), A("ident"), True, True, "g_b%d" % k)
-        cp("s", A("ya2", 128 * k, 128 * k + 128), A("ps%d" % (6 + k), 0, 128))
-        dma("y", ext(T["ya"][:, 1024 * k:1024 * k + 1024], "ya%d" % k), A("ya2", 128 * k, 128 * k + 128), "d_ya")
-    ts(A("r1"), A("ln", 16, 32), 9, OPS.arith_shift_right)
-    ts(A("r2"), A("ln", 16, 32), 31, OPS.bitwise_and)
-    ts(A("r5"), A("ln", 16, 32), 4, OPS.mult)
-    ts(A("r3"), A("r1"), -2016, OPS.mult)
-    ts(A("r4"), A("r2"), -3, OPS.mult)
-    tt(A("r6"), A("r5"), A("r3"), OPS.add)
-    tt(A("lbu"), A("r6"), A("r4"), OPS.add)
+    invert("l", 256)
+    new_a(1)
+    store("ya", "ya2", (6, 7))
+    cp("v", A("linv"), A("listl"))
 
     arrival("land6", 32, "arr6", calls3)
-    to_natural("land6", "q6", "ps2", "ps3")
-    cp("v", ind(A("w4"), A("lbu")), A("q6"))
-    for half in range(2):
-        ps = "ps%d" % half
-        for j in range(4):
-            for k in range(2):
-                lo = 1024 * k + 128 * (4 * half + j)
-                mm(A(ps, 32 * j + 16 * k, 32 * j + 16 * k + 16), A("w4", lo, lo + 128), A("i16", 0, 16), True, True,
-                   "g_yb%d" % half)
-        turn(A("yb2", 128 * half, 128 * half + 128), A(ps, 0, 128))
-    for h in range(8):
-        dma("ys"[h % 2], ext(T["yb"][:, 256 * h:256 * h + 256], "yb%d" % h), A("yb2", 0, 256, 16 * h, 16 * h + 16), "d_yb")
-    record("y", None, [], [(None, [("ext_ya%d" % h, 0, 128, 0, 1) for h in range(2)]
-                            + [("ext_yb%d" % h, 0, 128, 0, 1) for h in range(8)])])
+    for b in range(2):
+        mm(A("ps%d" % (2 + b), 0, 128), A("land6", b, 256, step=2), A("ident"), True, True, None)
+        cp("v", A("q6", 128 * b, 128 * b + 128), A("ps%d" % (2 + b), 0, 128))
+    for j0, j1 in ((0, 1), (1, 2), (2, 4), (4, 6), (6, 7), (7, 8)):
+        for e in range(2):
+            n = 8 * e + j0
+            add_groups("q6", ("linv", 8 * n), 128 * n,
+                       [A("ps%d" % (j // 4), 32 * (j % 4) + e, 32 * (j % 4) + 32, step=2) for j in range(j0, j1)],
+                       "vs"[e], "g_yb%d" % (j0 // 4))
+    store("yb", "yb2", (0, 1))
+    record("y", None, [], [(None, [("ext_%s%d" % (n, a), 0, 128, 0, 1) for n in ("ya", "yb") for a in range(4)])])
 
     bits = [0] * len(ops)
     known = {}
@@ -455,7 +520,7 @@ def rank_program(g, core, T, topo):
         o["waits"] = waits
         o["have"] = have
     needed_groups = set(ops[j]["grp"] for j in need if ops[j]["grp"] is not None)
-    chains, used, place, group_sem = [], [0], {}, {}
+    chains, used, where, group_sem = [], [0], {}, {}
 
     def fresh():
         used[0] += 1
@@ -463,11 +528,11 @@ def rank_program(g, core, T, topo):
 
     for k, o in enumerate(ops):
         if o["fixed"] is not None:
-            place[k] = o["fixed"]
+            where[k] = o["fixed"]
         elif o["grp"] in needed_groups and o["grp"] is not None:
             if o["grp"] not in group_sem:
                 group_sem[o["grp"]] = fresh()
-            place[k] = (group_sem[o["grp"]], sum(ops[m]["inc"] for m in groups[o["grp"]]))
+            where[k] = (group_sem[o["grp"]], sum(ops[m]["inc"] for m in groups[o["grp"]]))
         elif k in need:
             for c in chains:
                 if c["q"] == o["q"] and o["have"] >> c["last"] & 1:
@@ -477,7 +542,7 @@ def rank_program(g, core, T, topo):
                 chains.append(c)
             c["last"] = k
             c["n"] += o["inc"]
-            place[k] = (c["sem"], c["n"])
+            where[k] = (c["sem"], c["n"])
     assert used[0] <= NSEM, used[0]
 
     for k, o in enumerate(ops):
@@ -486,13 +551,13 @@ def rank_program(g, core, T, topo):
         q = queues[o["q"]]
         best = {}
         for j in o["waits"]:
-            s, v = place[j]
+            s, v = where[j]
             best[s] = max(v, best.get(s, 0))
         for s in sorted(best):
             q.wait_ge(T.sem[s], best[s])
         if o["f"] is None:
             continue
         x = o["f"]()
-        if k in place:
-            x.then_inc(T.sem[place[k][0]], o["inc"])
+        if k in where:
+            x.then_inc(T.sem[where[k][0]], o["inc"])
     g.wait_ge(T.sem["sent"], sent[0])

import numpy as np
from concourse.bass import DstId, RemoteDMATransfer
from concourse.mybir import AluOpType, ActivationFunctionType

OPS = AluOpType
COPY = ActivationFunctionType.Copy
F, BFT, I32, U16, F16 = "float32", "bfloat16", "int32", "uint16", "float16"

NDUMP = 640
SCRATCH = {}
for _n, _c, _t in [
        ("ia", 144, I32), ("iab", 128, I32), ("i2", 8, I32), ("i2b", 8, I32), ("i5", 128, I32), ("dj", 32, F),
        ("mk", 8, F), ("nm", 8, F), ("i16", 128, F), ("ident", 128, F), ("e8", 128, F), ("e8b", 128, BFT),
        ("idf", 8, F16), ("n1", 128, F16), ("zb", 144, BFT), ("zc", 144, BFT), ("pos", 512, BFT),
        ("repb", 1024, BFT), ("repf", 1024, F),
        ("tf", 2048, BFT), ("far", 2048, BFT), ("v8", 512, F), ("v16", 512, F), ("xi", 128, I32), ("ll", 32, I32),
        ("llh", 32, F16), ("lau", 16, U16), ("lu", 32, U16), ("lf", 128, U16), ("xu", 96, U16),
        ("r1", 32, I32), ("r2", 32, I32), ("r3", 32, I32), ("r4", 32, I32), ("r5", 32, I32), ("pli", 32, I32),
        ("pla", 16, U16), ("kl", 16, I32), ("ml", 16, F), ("nl", 16, F), ("offl", 16, U16),
        ("ka", 64, I32), ("ma", 64, F), ("na", 64, F), ("sa", 64, I32),
        ("ko", 32, I32), ("mo", 32, F), ("no", 32, F), ("obt", 32, U16),
        ("xa16", 32, F16), ("nea", 32, BFT), ("ga", 32, F), ("offa", 32, U16), ("rowa", 512, BFT),
        ("xb16", 32, F16), ("neb", 32, BFT), ("gb", 32, F), ("offb", 32, U16), ("rowb", 512, BFT),
        ("wina", 2048 + NDUMP, BFT), ("winb", 2048 + NDUMP, BFT), ("winc", 2048, BFT), ("winl", 2048, BFT),
        ("met", 2048, BFT), ("lista", 128, BFT), ("listb", 128, BFT), ("listc", 128, BFT), ("listl", 128, BFT),
        ("enda", 128, U16), ("endb", 128, U16), ("lcomp", 128, U16), ("linv", 128, U16),
        ("xr", 512, I32), ("gx", 512, F16), ("pk", 32, I32), ("xbo", 32, I32), ("xao", 32, I32), ("xaou", 32, U16),
        ("s1", 512, BFT), ("land1", 512, BFT), ("tb", 2048, BFT), ("tc", 2048, BFT), ("vc", 512, F), ("vcp", 512, F),
        ("wa", 512, F), ("ra", 520, F), ("s3", 256, F), ("q3", 264, F), ("fan", 256, F),
        ("w2", 2048, F), ("gt", 2048, F), ("ya2", 256, F),
        ("s5", 256, F), ("s5x", 512, F), ("land3", 256, F), ("land5", 256, F), ("land6", 256, F),
        ("ta", 2048, F), ("wb", 512, F), ("rb", 520, F), ("s6", 256, F), ("q6", 264, F), ("yb2", 256, F)]:
    SCRATCH[_n] = ("sbuf", [128, _c], _t)
SCRATCH["l8"] = ("sbuf", [128, 2, 16, 16], I32)
SCRATCH["l8h"] = ("sbuf", [128, 2, 16, 16], F16)
SCRATCH["idh"] = ("sbuf", [128, 8, 16], BFT)
for _k in range(8):
    SCRATCH["ps%d" % _k] = ("psum", [128, 512] if _k in (1, 5, 6) else [128, 2, 256], F)
NSEM = 130
SEMAPHORES = ["e%d" % k for k in range(NSEM)] + ["arr%d%s" % (k, s) for k in (1, 3, 5, 6) for s in "fhsn"] + ["sent"]


def rank_program(g, core, T, topo):
    me = T.rank_of(core)
    if me is None:
        return
    cores = list(T.cores)
    here = topo.chip(core)
    queues = {"v": g.vector, "s": g.scalar, "t": g.tensor, "g": g, "y": g.sync}

    ops = []
    hist = {}
    groups = {}

    def record(q, f, outs, ins, grp=None, inc=1, fixed=None):
        k = len(ops)
        dep = set()
        touched = []
        for w, side in ((1, outs), (0, ins)):
            for pair in side:
                for reg in pair[1]:
                    touched.append((w, reg))
        for w, reg in touched:
            n, a, b, lo, hi = reg
            for (j, w2, a2, b2, lo2, hi2) in hist.get(n, []):
                if n[:2] == "ps":
                    if ops[j]["q"] == q:
                        if q != "t" and (w or w2) and lo < hi2 and lo2 < hi:
                            dep.add(j)
                    else:
                        dep.add(j)
                elif (w or w2) and lo < hi2 and lo2 < hi and a < b2 and a2 < b:
                    dep.add(j)
        for w, reg in touched:
            hist.setdefault(reg[0], []).append((k, w) + tuple(reg[1:]))
        if grp is not None:
            groups.setdefault(grp, []).append(k)
        dep.discard(k)
        ops.append({"q": q, "f": f, "dep": dep, "grp": grp, "inc": inc, "fixed": fixed})
        return k

    def A(n, lo=0, hi=None, p0=0, p1=128, step=1):
        if n[:2] == "ps" and len(SCRATCH[n][1]) == 3:
            hi = 512 if hi is None else hi
            h = lo // 256
            ap = T[n][p0:p1, h, lo - 256 * h:hi - 256 * h:step] if hi <= 256 * h + 256 else T[n][p0:p1, :, lo:256:step]
            return (ap, [(n, p0, p1, lo, hi)])
        hi = SCRATCH[n][1][1] if hi is None else hi
        return (T[n][p0:p1, lo:hi] if step == 1 else T[n][p0:p1, lo:hi:step], [(n, p0, p1, lo, hi)])

    def X(ap, n, lo, hi):
        return (ap, [(n, 0, 128, lo, hi)])

    def rows(n, lo, hi, p0=0):
        return (T[n][p0:128:16, lo:hi], [(n, 0, 128, lo, hi)])

    def ind(win, off):
        return (win[0].indirect(off[0]), win[1] + off[1])

    def cp(q, out, in_, grp=None):
        if q == "v":
            record(q, lambda: g.vector.tensor_copy(out[0], in_[0]), [out], [in_], grp)
        else:
            record(q, lambda: g.scalar.activation(out[0], in_[0], COPY), [out], [in_], grp)

    def scaled(out, in_, s, grp=None):
        record("s", lambda: g.scalar.activation(out[0], in_[0], COPY, scale=s[0]), [out], [in_, s], grp)

    def constant(out, in_, c):
        record("s", lambda: g.scalar.activation(out[0], in_[0], ActivationFunctionType.Identity, bias=c, scale=0.0),
               [out], [in_])

    def tt(out, a, b, o, grp=None):
        record("v", lambda: g.vector.tensor_tensor(out[0], a[0], b[0], o), [out], [a, b], grp)

    def ts(out, a, s1, o1, s2=None, o2=None, grp=None):
        ins = [a] + [s for s in (s1, s2) if isinstance(s, tuple)]
        v1 = s1[0] if isinstance(s1, tuple) else s1
        v2 = s2[0] if isinstance(s2, tuple) else s2
        if o2 is None:
            record("v", lambda: g.vector.tensor_scalar(out[0], a[0], v1, None, o1), [out], ins, grp)
        else:
            record("v", lambda: g.vector.tensor_scalar(out[0], a[0], v1, v2, o1, o2), [out], ins, grp)

    def fill(out, c, grp=None):
        record("v", lambda: g.vector.memset(out[0], c), [out], [], grp)

    def turn(out, in_):
        record("v", lambda: g.vector.transpose(out[0], in_[0]), [out], [in_])

    def mm(out, l, r, start, stop, grp):
        record("t", lambda: g.tensor.matmul(out[0], l[0], r[0], start, stop), [out], [l, r], grp)

    def iota(n, pattern, base, cm, lo=0):
        out = A(n, lo)
        if SCRATCH[n][2] != I32:
            record("g", lambda: g.iota(out[0], pattern, base, cm, allow_small_or_imprecise_dtypes=True), [out], [])
        else:
            record("g", lambda: g.iota(out[0], pattern, base, cm), [out], [])

    def scan(out, keep, x):
        record("v", lambda: g.vector.tensor_tensor_scan(out[0], keep[0], x[0], 0.0, OPS.mult, OPS.add), [out], [keep, x])

    def dma(q, out, in_, grp, after=()):
        e = queues[q]
        record(q, lambda: e.dma_start(out[0], in_[0]), [out], [in_] + list(after), grp, 16)

    def ext(ap, n):
        return (ap, [("ext_" + n, 0, 128, 0, 1)])

    ranks = range(len(cores))

    def chip(q):
        return topo.chip(cores[q])

    def row(q):
        return len([p for p in ranks if p < q and topo.same_plane(chip(p), chip(q))])

    sib = [q for q in ranks if q != me and chip(q) == here]
    near = [q for q in ranks if topo.same_plane(chip(q), here)]
    others = [q for q in ranks if q != me and q not in sib and q not in near]
    far0 = [q for q in others if row(q) == row(me)]
    far1 = [q for q in others if q not in far0]
    p_own, p_far0, p_far1, p_near = min(sib + [me]), min(far0), min(far1), min(near)
    kinds = (("s", sib), ("f", far0), ("h", far1), ("n", near))

    off_chip = topo.engines(core, cores[others[0]])
    on_chip = [e for e in topo.engines(core, cores[sib[0]]) if e not in off_chip]

    def engines_for(q, dests):
        if q in sib:
            return on_chip[:len(on_chip) // 2]
        dests = [d for d in dests if d not in sib]
        n = len(off_chip) // len(dests)
        i = dests.index(q)
        return off_chip[i * n:(i + 1) * n]

    sent = [0]

    def send(src, width, dst, arr, dests):
        tr, rd = [], []
        for q in dests:
            lo = q * width % SCRATCH[src][1][1]
            s = A(src, lo, lo + width)
            rd.append(s)
            rid, pid = topo.addr(cores[q])[:2]
            es = engines_for(q, dests)
            sent[0] += len(es)
            w = [k for k, qs in kinds if q in qs][0]
            tr.append(RemoteDMATransfer(dst_ids=[DstId(rid=rid, pnc=pid)], dma_engine_mask=sum(1 << e for e in es),
                                        remote_sem=T.sem[arr + w], srcs=[s[0]],
                                        dsts=[T[dst][:, width * me:width * me + width]]))
        record("g", lambda: g.remote_dma_fused(tr, local_sem=T.sem["sent"]), [], rd)

    def arrival(n, width, arr, calls, own=None):
        for w, srcs in kinds:
            m, c = own if own and srcs is sib else (n, width)
            regs = [(m, 0, 128, q * c, (q + 1) * c) for q in srcs]
            num = sum(len(engines_for(q, dests)) for dests in calls for q in dests if q in srcs)
            record("in_" + arr + w, None, [(None, regs)], [], fixed=(arr + w, num))

    calls1 = (sib, far0, far1, near)
    calls3 = (far0, far1, near, sib)

    for k, n in enumerate(("lc", "lb")):
        dma("ys"[k], X(T["l8"][0:8, k, :, :], "l8", k, k + 1), ext(T[n][:, :], n), "d_l")
    dma("s", A("v8", 0, 512, 0, 8), ext(T["v"][:, :], "v"), None)
    for k in range(8):
        n = "fb" if k % 2 else "fc"
        dma("ys"[k % 2], A("tf", 0, 2048, 16 * k, 16 * k + 16), ext(T[n][:, :], n), "d_tf")
    for k, n in enumerate(("xa", "xb")):
        dma("ys"[k], A("xi", 32 * k, 32 * k + 32), ext(T[n][:, :], n), None)
    dma("y", A("ll", 16, 32), ext(T["la"][:, :], "la"), None)
    for k, n in ((2, "xc"), (3, "ob")):
        dma("y", A("xi", 32 * k, 32 * k + 32), ext(T[n][:, :], n), "d_x")

    iota("ia", [[1, 144]], 0, -1)
    iota("i2", [[-16, 8]], 0, 1)
    iota("i5", [[1, 8], [0, 16]], 0, -1)
    iota("dj", [[16, 32]], 2048, 1)
    iota("pos", [[1, 512]], -256, 0)
    fill(A("winc", 0, 768), 256.0)
    for s in "abl":
        dma("y", rows("win" + s, 0, 2048), A("winc", 0, 512, 0, 32), None)
    ts(A("iab"), A("ia", 0, 128), 15, OPS.bitwise_and)
    ts(A("i2b"), A("i2"), 4, OPS.arith_shift_right)
    ts(A("i16"), A("iab"), 0, OPS.is_equal)
    ts(A("mk"), A("i2b"), 0, OPS.is_equal)
    ts(X(T["idh"][:, :, :], "idh", 0, 128), A("ia", 0, 128), 0, OPS.is_equal)
    ts(A("e8"), A("i5"), 0, OPS.is_equal)
    for h in range(8):
        scaled(A("repb", 128 * h, 128 * h + 128), A("i16"), A("mk", h, h + 1), "g_repb")

    ts(A("nm", 0, 1), A("i16", 0, 1), 0, OPS.is_equal)
    ts(A("zb"), A("ia"), 15, OPS.is_equal, A("i16", 0, 1), OPS.mult)
    ts(A("idf"), A("ia", 0, 8), 0, OPS.is_equal)
    cp("v", X(T["l8h"][0:8, :, :, :], "l8h", 0, 2), X(T["l8"][0:8, :, :, :], "l8", 0, 2))
    for k in range(16):
        mm(A("ps4", k % 4, 32, 32 * (k // 4), 32 * (k // 4) + 32, 4), X(T["l8h"][0:8, :, :, k], "l8h", 0, 2),
           A("idf", 0, 8, 0, 8), True, True, "g_lt")
    mm(A("ps5"), A("e8", 0, 128, 0, 8), A("v8", 0, 512, 0, 8), True, True, "g_v")
    ts(A("n1"), A("ia", 0, 128), -1, OPS.is_equal, A("nm", 0, 1), OPS.mult)
    cp("v", A("lu"), A("ps4", 0, 32))
    cp("s", A("e8b"), A("e8"))
    ts(A("nm", 1, 2), A("i16", 1, 2), 2048, OPS.mult, A("i16", 0, 1), OPS.add)
    ts(A("nm", 2, 3), A("i16", 1, 2), -1, OPS.mult, 15, OPS.add)
    ts(A("zc"), A("ia"), A("nm", 2, 3), OPS.is_equal, A("nm", 1, 2), OPS.mult)
    for e, p in (("v", p_far0), ("s", p_own), ("v", p_far1), ("s", p_near)):
        cp(e, A("s1", 64 * p, 64 * p + 128), ind(A("tf"), A("lu", 4 * p, 4 * p + 8)))
    for dests in calls1:
        send("s1", 64, "land1", "arr1", dests)
    cp("s", A("land1", 64 * me, 64 * me + 64), A("s1", 64 * me, 64 * me + 64))
    iota("xr", [[0, 512]], 0, 0)
    for n, lo in (("ra", 512), ("rb", 512), ("q3", 256), ("q6", 256)):
        iota(n, [[0, 8]], 0, 0, lo)
    iota("w2", [[0, 2048]], 0, 0)

    def following(x, ps, s):
        mm(A(ps, 0, 32), A("n1"), A(x, 0, 32), True, False, "g_n" + s)
        mm(A(ps, 0, 31), A("zb", 0, 128), A(x, 1, 32), False, True, "g_n" + s)

    def by_rows(x, s, out, n=128):
        ts(A("k" + s), x, 4, OPS.arith_shift_right)
        ts(A("m" + s), x, n, OPS.mult)
        ts(A("n" + s), A("k" + s), 1 - 16 * n, OPS.mult)
        tt(A(out), A("m" + s), A("n" + s), OPS.add)

    def ends(x, place, ps, s):
        tt(A("ne" + s), A(ps, 0, 32), A(x), OPS.is_equal)
        tt(A("g" + s), A("dj"), A("ne" + s), OPS.mult)
        dma("y", A("row" + s, 0, 512, 0, 8), A("ne" + s), None)
        tt(A("off" + s), A("g" + s), place, OPS.max)

    def invert(s, lo=0):
        cp("v", ind(A("win" + s), A("off" + s)), A("pos", lo, 512))
        dma("y", A("list" + s), rows("win" + s, 0, 2048), None)

    def keep(ps, s):
        for i in range(16):
            lo = 32 * (i - 1) if i else 479
            mm(A(ps, i, 512, step=16), A("e8b", 0, 128, 0, 8), A("row" + s, lo, lo + 32, 0, 8), True, True, "g_k" + s)

    def table(f, q, n, k, e):
        for i in range(4 * n):
            w = 128 * (2 * (i % 4) + f)
            lo = 64 * (q + i // 4)
            mm(A("ps%d" % k, 64 * i, 64 * i + 64), A("repb", w, w + 128), A("land1", lo, lo + 64), True, True,
               "g_t%d%d%d" % (f, k, q))
        cp(e, A("tb" if f else "tc", 256 * q, 256 * (q + n)), A("ps%d" % k, 0, 256 * n))

    ts(A("xa16"), A("xi", 0, 32), 1, OPS.add)
    following("xa16", "ps7", "a")
    by_rows(A("xi", 0, 64), "a", "sa")
    ends("xa16", A("sa", 0, 32), "ps7", "a")
    for k in range(2):
        cp("v", A("llh", 16 * k, 16 * k + 16), A("ll", 16, 32), "g_lah")
    invert("a")
    constant(A("winc", 768, 2048), A("tf", 768, 2048), 256.0)
    table(0, me, 1, 0, "s")
    table(1, me, 1, 4, "s")
    cp("s", A("v16"), A("ps5"))
    cp("s", A("ident"), X(T["idh"][:, :, :], "idh", 0, 128))
    cp("s", A("repf", 0, 512), A("repb", 0, 512))
    cp("v", A("lau"), A("ll", 16, 32))
    chips5 = (p_far0, p_far1, p_near, p_own)
    parts = ((0, 5), (5, 8))
    for lo, hi in parts:
        for d in range(lo, hi):
            r = chips5[d // 2] + d % 2
            for a in range(4):
                mm(A("ps6", 16 * lo + d - lo, 16 * hi, 32 * a, 32 * a + 32, hi - lo), A("llh"),
                   X(T["idh"][:, r, :], "idh", 0, 128), True, True, "g_lf")
    cp("v", ind(A("winc"), A("lau")), A("pos", 256, 512))
    cp("v", A("lf"), A("ps6", 0, 128))
    cp("v", A("xu"), A("xi", 32, 128))
    by_rows(A("xi", 96, 128), "o", "obt", 32)

    arrival("land1", 64, "arr1", calls1)
    through = [A("land1", 64 * q, 64 * q + 64) for q in near]
    dma("y", rows("xr", 0, 512), ext(T["xa"][:, :], "xa"), "d_xr", through)
    dma("y", rows("xr", 0, 512, 1), A("sa", 32, 64), "d_xr", through)
    dma("y", A("ll", 0, 16), ext(T["lb"][:, :], "lb"), None, through)
    for k in range(8):
        dma("y", A("far", 0, 2048, 16 * k, 16 * k + 16), ext(T["fa"][:, :], "fa"), "d_fa", through)
    table(0, sib[0], 1, 0, "s")
    table(1, sib[0], 1, 4, "s")
    table(0, p_far0, 2, 1, "v")
    table(1, p_far0, 2, 5, "s")
    table(0, p_far1, 2, 2, "v")
    table(1, p_far1, 2, 6, "s")
    table(0, p_near, 1, 3, "v")
    table(0, p_near + 1, 1, 0, "s")
    table(1, p_near, 2, 7, "s")
    keep("ps1", "a")
    tt(A("vc"), ind(A("tc"), A("xu", 32, 64)), A("v16"), OPS.mult)

    def meet(d):
        lo, hi = parts[d]
        cp("s", A("met", 256 * lo, 256 * hi), ind(A("winc"), A("lf", 16 * lo, 16 * hi)))
        dma("y", A("listc", 16 * lo, 16 * hi), rows("met", 256 * lo, 256 * hi), None)

    def meet_list(d):
        lo, hi = parts[d]
        cp("v", A("lcomp", 16 * lo, 16 * hi), A("listc", 16 * lo, 16 * hi))

    meet(0)
    tt(A("wa"), ind(A("tb"), A("xu", 0, 32)), A("vc"), OPS.mult)
    ts(A("enda"), A("lista"), 256, OPS.add)
    scan(A("ra", 0, 512), A("ps1"), A("wa"))

    def add_groups(win, lst, col, out, e, grp):
        cp(e, A("gt", col, col + 128 * len(out)), ind(A(win), A(lst[0], lst[1], lst[1] + 8 * len(out))))
        for b, o in enumerate(out):
            mm(o, A("gt", col + 128 * b, col + 128 * b + 128), A("i16", 0, 16), True, True, grp)

    def add_slabs(win, lst, s, land, arr):
        def part(q, k, e, lo=0, hi=2):
            c = 32 * (q % 2)
            out = [A("ps%d" % k, c + b, c + 32, step=2) for b in range(lo, hi)]
            add_groups(win, (lst, 16 * q + 8 * lo), 256 * q + 128 * lo, out, e, "g_%s%d%d" % (win, k, q == me))

        def out(p, n, k, e, call):
            cp(e, A(s, 32 * p, 32 * (p + n)), A("ps%d" % k, 32 * (p % 2), 32 * (p % 2 + n)))
            send(s, 32, land, arr, calls3[call])

        for b in range(2):
            part(far0[0], 0, "v", b, b + 1)
            part(far0[1], 0, "s", b, b + 1)
        part(far1[0], 1, "v")
        part(far1[1], 1, "s")
        out(p_far0, 2, 0, "v", 0)
        part(near[0], 2, "s")
        part(near[1], 2, "v")
        out(p_far1, 2, 1, "s", 1)
        part(sib[0], 3, "v")
        part(me, 0, "s")
        out(p_near, 2, 2, "v", 2)
        out(sib[0], 1, 3, "v", 3)
        cp("s", A(land, 32 * me, 32 * me + 32), A("ps0", 32 * (me % 2), 32 * (me % 2) + 32))

    add_slabs("ra", "enda", "s3", "land3", "arr3")

    cp("s", A("fan"), ind(A("far"), A("lau")))
    meet(1)
    cp("s", A("repf", 512, 1024), A("repb", 512, 1024))
    cp("v", A("gx"), ind(A("xr"), A("obt")))
    for i in range(16):
        mm(A("ps5", 0, 32), A("zc", 15 - i, 143 - i), A("gx", i, 512, step=16), i == 0, i == 15, "g_pk")
    meet_list(0)
    ts(A("r1"), A("ll"), 480, OPS.bitwise_and)
    ts(A("r2"), A("ll"), 511, OPS.bitwise_and)
    ts(A("r3"), A("ll"), 4, OPS.arith_shift_right, 96, OPS.bitwise_and)
    ts(A("r4"), A("r1"), 3, OPS.mult)
    tt(A("r5"), A("r2"), A("r3"), OPS.add)
    tt(A("pli"), A("r5"), A("r4"), OPS.add)
    cp("v", A("pk"), A("ps5", 0, 32))
    ts(A("xbo"), A("pk"), 11, OPS.arith_shift_right)
    ts(A("xao"), A("pk"), 2047, OPS.bitwise_and)
    ts(A("xb16"), A("xbo"), 1, OPS.add)

    arrival("land3", 32, "arr3", calls3)
    for b in range(2):
        mm(A("ps%d" % (6 + b), 0, 128), A("land3", b, 256, step=2), A("ident"), True, True, None)
        tt(A("q3", 128 * b, 128 * b + 128), A("ps%d" % (6 + b), 0, 128), A("fan", 128 * b, 128 * b + 128), OPS.mult)
    following("xb16", "ps5", "b")

    def part5(q, k, e, halves=False):
        c = 32 * (q % 2)
        out = [A("ps%d" % k, c + 16 * b, c + 16 * b + 16) for b in range(2)]
        for lo, hi in ((0, 1), (1, 2)) if halves else ((0, 2),):
            add_groups("q3", ("lcomp", 32 * chips5.index(q - q % 2) + 16 * (q % 2) + 8 * lo), 256 * q + 128 * lo,
                       out[lo:hi], e[lo], "g_m%d" % k)

    def out5(p, n, k, call):
        turn(A("s5", 32 * p, 32 * (p + n)), A("ps%d" % k, 32 * (p % 2), 32 * (p % 2 + n)))
        send("s5", 32, "land5", "arr5", calls3[call])

    def whole(q, k, e, out):
        d = 6 + q % 2
        cp(e, A("gt", 256 * q, 256 * q + 256), ind(A("q3"), A("lcomp", 16 * d, 16 * d + 16)))
        mm(A("ps%d" % k, 0, 256), A("i16"), A("gt", 256 * q, 256 * q + 256), True, True, None)
        cp("s", out, A("ps%d" % k, 0, 256))

    part5(far0[0], 0, "vs", True)
    part5(far0[1], 0, "vs", True)
    part5(far1[0], 1, "v")
    part5(far1[1], 1, "s")
    out5(p_far0, 2, 0, 0)
    meet_list(1)
    part5(near[0], 2, "s")
    part5(near[1], 2, "v")
    out5(p_far1, 2, 1, 1)
    whole(sib[0], 3, "s", A("s5x", 256 * (sib[0] % 2), 256 * (sib[0] % 2) + 256))
    out5(p_near, 2, 2, 2)
    send("s5x", 256, "ta", "arr5", sib)
    whole(me, 4, "v", A("ta", 256 * me, 256 * me + 256))

    ends("xb16", A("xbo"), "ps5", "b")
    invert("b")
    cp("v", A("pla"), A("pli", 16, 32))
    cp("v", A("xaou"), A("xao"))
    by_rows(A("pli", 0, 16), "l", "offl")
    cp("v", ind(A("w2"), A("pla")), A("q3", 0, 256))

    arrival("land5", 32, "arr5", calls3, ("ta", 256))
    cp("s", A("vcp"), ind(A("vc"), A("xu", 64, 96)))
    for q, k, u0, u1, e in ((p_far0, 7, 0, 8, "s"), (p_far1, 0, 0, 8, "s"),
                            (p_near, 4, 0, 4, "s"), (p_near, 3, 4, 6, "v"), (p_near, 2, 6, 8, "v")):
        for u in range(u0, u1):
            h = 2 * (u % 4) + u // 4
            mm(X(T["ps%d" % k][:, :, 32 * u:32 * u + 32], "ps%d" % k, 0, 512), A("repf", 128 * h, 128 * h + 128),
               A("land5", 32 * q, 32 * q + 64), True, True, "g_u%d" % k)
        if u1 - u0 == 8:
            cp(e, A("ta", 256 * q, 256 * q + 512), A("ps%d" % k))
        else:
            for w in range(2):
                lo, hi = 256 * w + 32 * u0, 256 * w + 32 * u1
                cp(e, A("ta", 256 * q + lo, 256 * q + hi), A("ps%d" % k, lo, hi))
        if k == 0:
            ts(A("endb"), A("listb"), 256, OPS.add)
    keep("ps5", "b")

    def new_a(half):
        for j in range(4):
            for e in range(2):
                lo = 128 * (8 * e + 4 * half + j)
                mm(A("ps%d" % (6 + half), 32 * j + e, 32 * j + 32, step=2), A("w2", lo, lo + 128), A("i16", 0, 16),
                   True, True, "g_ya%d" % half)

    def store(n, s, banks):
        for k in range(2):
            turn(A(s, 128 * k, 128 * k + 128), A("ps%d" % banks[k], 0, 128))
        for a in range(4):
            dma("ys"[a % 2] if n == "yb" else "y", ext(T[n][:, 512 * a:512 * a + 512], "%s%d" % (n, a)),
                A(s, 0, 256, 32 * a, 32 * a + 32), "d_" + n)

    new_a(0)
    tt(A("wb"), ind(A("ta"), A("xaou")), A("vcp"), OPS.mult)
    scan(A("rb", 0, 512), A("ps5"), A("wb"))

    add_slabs("rb", "endb", "s6", "land6", "arr6")

    invert("l", 256)
    new_a(1)
    store("ya", "ya2", (6, 7))
    cp("v", A("linv"), A("listl"))

    arrival("land6", 32, "arr6", calls3)
    for b in range(2):
        mm(A("ps%d" % (2 + b), 0, 128), A("land6", b, 256, step=2), A("ident"), True, True, None)
        cp("v", A("q6", 128 * b, 128 * b + 128), A("ps%d" % (2 + b), 0, 128))
    for j0, j1 in ((0, 1), (1, 2), (2, 4), (4, 6), (6, 7), (7, 8)):
        for e in range(2):
            n = 8 * e + j0
            add_groups("q6", ("linv", 8 * n), 128 * n,
                       [A("ps%d" % (j // 4), 32 * (j % 4) + e, 32 * (j % 4) + 32, step=2) for j in range(j0, j1)],
                       "vs"[e], "g_yb%d" % (j0 // 4))
    store("yb", "yb2", (0, 1))
    record("y", None, [], [(None, [("ext_%s%d" % (n, a), 0, 128, 0, 1) for n in ("ya", "yb") for a in range(4)])])

    bits = [0] * len(ops)
    known = {}
    need = set()
    for k, o in enumerate(ops):
        have = known.get(o["q"], 0)
        waits = []
        for j in sorted(o["dep"], reverse=True):
            if have >> j & 1:
                continue
            members = groups[ops[j]["grp"]] if ops[j]["grp"] is not None else [j]
            if k in members:
                continue
            assert max(members) < k
            for m in members:
                have |= bits[m]
            waits.append(j)
            need.add(j)
        known[o["q"]] = have
        bits[k] = have | 1 << k
        o["waits"] = waits
        o["have"] = have
    needed_groups = set(ops[j]["grp"] for j in need if ops[j]["grp"] is not None)
    chains, used, where, group_sem = [], [0], {}, {}

    def fresh():
        used[0] += 1
        return "e%d" % (used[0] - 1)

    for k, o in enumerate(ops):
        if o["fixed"] is not None:
            where[k] = o["fixed"]
        elif o["grp"] in needed_groups and o["grp"] is not None:
            if o["grp"] not in group_sem:
                group_sem[o["grp"]] = fresh()
            where[k] = (group_sem[o["grp"]], sum(ops[m]["inc"] for m in groups[o["grp"]]))
        elif k in need:
            for c in chains:
                if c["q"] == o["q"] and o["have"] >> c["last"] & 1:
                    break
            else:
                c = {"q": o["q"], "sem": fresh(), "last": None, "n": 0}
                chains.append(c)
            c["last"] = k
            c["n"] += o["inc"]
            where[k] = (c["sem"], c["n"])
    assert used[0] <= NSEM, used[0]

    for k, o in enumerate(ops):
        if o["fixed"] is not None:
            continue
        q = queues[o["q"]]
        best = {}
        for j in o["waits"]:
            s, v = where[j]
            best[s] = max(v, best.get(s, 0))
        for s in sorted(best):
            q.wait_ge(T.sem[s], best[s])
        if o["f"] is None:
            continue
        x = o["f"]()
        if k in where:
            x.then_inc(T.sem[where[k][0]], o["inc"])
    g.wait_ge(T.sem["sent"], sent[0])
